import numpy as np
import ml_dtypes


def mxq(x, axis, fmt="e4m3"):
    dtype, down = {"e4m3": (ml_dtypes.float8_e4m3fn, 7), "e5m2": (ml_dtypes.float8_e5m2, 14)}[fmt]
    v = np.moveaxis(np.asarray(x, np.float32).astype(ml_dtypes.bfloat16).astype(np.float64), axis, -1)
    blocks = v.reshape(v.shape[:-1] + (-1, 32))
    amax = np.abs(blocks).max(-1, keepdims=True)
    byte = np.maximum(np.where(amax > 0, np.frexp(amax)[1] - 1 + 127, 0) - down, 1)
    scale = np.exp2(byte - 127.0)
    codes = (blocks / scale).astype(np.float32).astype(dtype).astype(np.float64)
    return np.moveaxis((codes * scale).reshape(v.shape), -1, axis)


WIDE = False


def mx_kscale(k):
    if not WIDE:
        return np.ones(k)
    levels = np.array([10, -10, 5, -5, 0])
    if k % 512:
        return np.exp2(np.random.permutation(np.resize(levels, k // 32))).repeat(32)
    a = np.empty((k // 512, 16))
    for p in range(k // 512):
        a[p, :8] = np.random.permutation(np.resize(levels, 8))
        for g in range(8):
            far = levels[np.abs(levels - a[p, g]) >= 10]
            a[p, g + 8] = far[np.random.randint(len(far))]
    return np.exp2(a.ravel()).repeat(32)


BF16 = ml_dtypes.bfloat16


def bf(x):
    return np.asarray(x, np.float32).astype(BF16)


def f64(x):
    return np.asarray(x).astype(np.float64)


E2M1 = np.array([0.0, 0.5, 1.0, 1.5, 2.0, 3.0, 4.0, 6.0, -0.0, -0.5, -1.0, -1.5, -2.0, -3.0, -4.0, -6.0])


def pack_weight(w, fmt):
    k, n = w.shape
    w = f64(bf(w)).reshape(k // 32, 32, n)
    amax = np.abs(w).max(1)
    if fmt == "e4m3":
        byte = np.frexp(amax)[1] - 1 + 127 - 7
    else:
        mant, ex = np.frexp(amax / 6.0)
        byte = np.where(mant > 0.5, ex, ex - 1) + 127
    byte = np.clip(np.where(amax > 0, byte, 1), 1, 254)
    scaled = (w * np.exp2(127.0 - byte)[:, None, :]).reshape(k, n).astype(np.float32)
    by_word = np.ascontiguousarray(scaled.reshape(k // 512, 128, 4, n).transpose(0, 1, 3, 2))
    if fmt == "e4m3":
        words = by_word.astype(ml_dtypes.float8_e4m3fn).view(np.uint8)
    else:
        c = by_word.astype(ml_dtypes.float4_e2m1fn).view(np.uint8) & 0xF
        words = c[..., 0::2] | (c[..., 1::2] << 4)
    return np.ascontiguousarray(words), np.ascontiguousarray(byte.astype(np.uint8).reshape(k // 512, 16, n))


def unpack_weight(words, scales, fmt):
    g, p, n, _ = words.shape
    if fmt == "e4m3":
        vals = np.ascontiguousarray(words).view(ml_dtypes.float8_e4m3fn).astype(np.float64)
    else:
        nib = np.empty((g, p, n, 4), np.uint8)
        nib[..., 0::2] = words & 0xF
        nib[..., 1::2] = words >> 4
        vals = E2M1[nib]
    vals = vals * np.repeat(np.exp2(scales.astype(np.float64) - 127.0), 8, axis=1)[..., None]
    return vals.transpose(0, 1, 3, 2).reshape(g * 512, n)
def pack4(w):
    words, scales = pack_weight(w, "e2m1")
    return words.reshape(words.shape[0], 128, -1), scales


def unpack4(words, scales):
    return unpack_weight(words.reshape(words.shape[0], 128, -1, 2), scales, "e2m1")


def planes(Y):
    n, m = Y.shape
    b = f64(bf(Y)).reshape(n // 32, 32, m)
    amax = np.abs(b).max(1)
    byte = np.clip(np.where(amax > 0, np.frexp(amax)[1] - 1 + 127 - 7, 1), 1, 254)
    codes = (b * np.exp2(127.0 - byte)[:, None, :]).reshape(n, m).astype(np.float32).astype(ml_dtypes.float8_e4m3fn).view(np.uint8)
    words = codes.reshape(n // 512, 128, 4, m).transpose(0, 1, 3, 2)
    return np.ascontiguousarray(words), np.ascontiguousarray(byte.astype(np.uint8).reshape(n // 512, 16, m))


T, D, B, V = 1024, 2048, 1024, 2048


def setup_inputs():
    s = mx_kscale(D)
    t = mx_kscale(B)
    h_words, h_scales = pack4(np.random.randn(D, T) * s[:, None])
    w_words, w_scales = pack4(1.5 * np.random.randn(D, B) / np.sqrt(D) / s[:, None])
    bit_weight = np.exp(0.3 * np.random.randn(B)) * t
    signs = np.where(np.random.randn(B, V) > 0, 1.0, -1.0)
    code = signs * np.exp(0.3 * np.random.randn(B, V)) / np.sqrt(B) / t[:, None]
    return {"h_words": h_words, "h_scales": h_scales, "w_words": w_words, "w_scales": w_scales,
            "bit_weight": bf(bit_weight), "code": bf(code),
            "token_scale": bf(np.exp(0.8 * np.random.randn(V))),
            "token_bias": bf(0.5 * np.random.randn(V))}

def reference(h_words, h_scales, w_words, w_scales, bit_weight, code, token_scale, token_bias):
    H = unpack4(h_words, h_scales)
    W = unpack4(w_words, w_scales)
    Z = H.T @ W
    L = -np.log(1.0 + np.exp(-Z)) * f64(bit_weight)
    S = mxq(L, 1, "e4m3") @ mxq(f64(code), 0, "e4m3")
    y = S * f64(token_scale) + f64(token_bias)
    Y = y.T
    words, scales = planes(Y)
    return y, words, scales

@@ -1,0 +1,357 @@
+from contextlib import ExitStack
+
+import concourse.mybir as mybir
+from concourse.masks import make_identity
+
+T, D, B, V = 1024, 2048, 1024, 2048
+FLOPS = 2 * T * D * B + 2 * T * B * V
+
+F32 = mybir.dt.float32
+BF16 = mybir.dt.bfloat16
+I32 = mybir.dt.int32
+U32 = mybir.dt.uint32
+U8 = mybir.dt.uint8
+FP8X4 = mybir.dt.float8_e4m3fn_x4
+FP4X4 = mybir.dt.float4_e2m1fn_x4
+ACT = mybir.ActivationFunctionType
+ALU = mybir.AluOpType
+
+P = 128
+N = 512
+SLOTS = 4
+D_PASSES = D // N
+B_PASSES = B // N
+V_GROUPS = V // N
+HALVES = T // N
+SOFT_BUFS = 12
+FLOOR = 2.0 ** -58
+WIDE_BUFS = 6
+CGRP_BUFS = 3
+
+
+def tile_signed_bit_code_scores_k5_kernel(
+    tc, h_words, h_scales, w_words, w_scales, bit_weight, code, token_scale, token_bias, out_0, out_1, out_2
+):
+    nc = tc.nc
+    with ExitStack() as ctx:
+        keep = ctx.enter_context(tc.tile_pool(name="keep", bufs=1))
+        work = ctx.enter_context(tc.tile_pool(name="work", bufs=2))
+        psum = ctx.enter_context(tc.psum_pool(name="psum", bufs=8))
+        ctx.enter_context(tc.manual_schedule())
+
+        def kept(name, shape, dtype):
+            return keep.tile(shape, dtype, name=name, align_bytes=64)
+
+        def bank():
+            return psum.tile([P, N], F32, name="bank")
+
+        w_raw = [kept("w_raw%d" % g, [P, D_PASSES, 2 * N], U8) for g in range(B_PASSES)]
+        ws_raw = [kept("ws_raw%d" % g, [P, D_PASSES, N], U8) for g in range(B_PASSES)]
+        w_ord = [kept("w_ord%d" % g, [P, D_PASSES, 2 * N], U8) for g in range(B_PASSES)]
+        ws_ord = [kept("ws_ord%d" % g, [P, D_PASSES, N], U8) for g in range(B_PASSES)]
+        h_w = [kept("h_w%d" % h, [P, D_PASSES, 2 * N], U8) for h in range(HALVES)]
+        h_s = [kept("h_s%d" % h, [P, D_PASSES, N], U8) for h in range(HALVES)]
+        c_raw = {}
+        for u in range(2):
+            for g in range(B_PASSES):
+                c_raw[g, u] = work.tile([P, SLOTS, V // 2], BF16, name="c_raw", tag="wide", bufs=WIDE_BUFS)
+        c_q = [[kept("c_q%d_%d" % (g, v), [P, N], U32) for v in range(V_GROUPS)] for g in range(B_PASSES)]
+        c_s = [[kept("c_s%d_%d" % (g, v), [P, N], U8) for v in range(V_GROUPS)] for g in range(B_PASSES)]
+        l_q = [[kept("l_q%d_%d" % (h, g), [P, N], U32) for g in range(B_PASSES)] for h in range(HALVES)]
+        l_s = [[kept("l_s%d_%d" % (h, g), [P, N], U8) for g in range(B_PASSES)] for h in range(HALVES)]
+        y_s = [kept("y_s%d" % h, [P, N], U8) for h in range(HALVES)]
+        ident = kept("ident", [P, P], F32)
+        bw_rows = kept("bw_rows", [P, P], BF16)
+        bw_rows32 = kept("bw_rows32", [P, P], F32)
+        bw_pos = kept("bw_pos", [P, B_PASSES * SLOTS], F32)
+        scale16 = kept("scale16", [P, V_GROUPS, SLOTS], BF16)
+        bias16 = kept("bias16", [P, V_GROUPS, SLOTS], BF16)
+        scale32 = kept("scale32", [P, V_GROUPS, SLOTS], F32)
+        bias32 = kept("bias32", [P, V_GROUPS, SLOTS], F32)
+        warm_in = kept("warm_in", [P, 1], F32)
+        warm_out = kept("warm_out", [P, 1], F32)
+
+        def load_words(dst, src, i):
+            view = src[:, :, 2 * N * i : 2 * N * (i + 1)].rearrange("g p b -> p g b")
+            nc.sync.dma_start(out=dst[:].bitcast(I32), in_=view.bitcast(I32))
+
+        def load_scales(dst, src, i, quadrants=range(4), queue=nc.sync):
+            for q in quadrants:
+                view = src[:, 4 * q : 4 * q + 4, N * i : N * (i + 1)].rearrange("g r n -> r g n")
+                queue.dma_start(out=dst[32 * q : 32 * q + 4, :, :].bitcast(I32), in_=view.bitcast(I32))
+
+        def load_code(g, u):
+            rows = code[N * g : N * (g + 1), (V // 2) * u : (V // 2) * (u + 1)]
+            rows = rows.rearrange("(q t r) v -> t q r v", t=SLOTS, r=8)
+            for t in range(SLOTS):
+                nc.sync.dma_start(out=c_raw[g, u][:, t, :], in_=rows[t])
+
+        def order_w(g):
+            nc.vector.tensor_copy(
+                out=ws_ord[g][:].bitcast(I32).rearrange("p a (t q w) -> p a t q w", t=SLOTS, q=16),
+                in_=ws_raw[g][:].bitcast(I32).rearrange("p a (q t w) -> p a t q w", t=SLOTS, q=16),
+            )
+            nc.vector.tensor_copy(
+                out=w_ord[g][:].bitcast(I32).rearrange("p a (t q w) -> p a t q w", t=SLOTS, q=16),
+                in_=w_raw[g][:].bitcast(I32).rearrange("p a (q t w) -> p a t q w", t=SLOTS, q=16),
+            )
+
+        grouped = {}
+
+        def code_group(g, v, on_gpsimd=False, on_scalar=False):
+            grouped["c", g, v] = work.tile([P, SLOTS * N], BF16, name="c_grp", align_bytes=64, bufs=CGRP_BUFS)
+            src = c_raw[g, v // 2][:, :, N * (v % 2) : N * (v % 2 + 1)].rearrange("p j (m s) -> p s m j", s=SLOTS)
+            dst = grouped["c", g, v][:].rearrange("p (s m j) -> p s m j", s=SLOTS, j=SLOTS)
+            if on_gpsimd:
+                nc.gpsimd.tensor_scalar(out=dst, in0=src, scalar1=1.0, scalar2=0.0, op0=ALU.mult, op1=ALU.add)
+            elif on_scalar:
+                nc.scalar.copy(out=dst, in_=src)
+            else:
+                nc.vector.tensor_copy(out=dst, in_=src)
+
+        def code_quant(g, v):
+            nc.vector.quantize_mx(out=c_q[g][v][:].bitcast(FP8X4), scales=c_s[g][v][:], in_=grouped["c", g, v][:])
+
+        logits = {}
+        soft = {}
+        l16 = {}
+
+        def logit_mm(h, g, t):
+            z = bank()
+            logits[h, g, t] = z
+            for a in range(D_PASSES):
+                nc.tensor.matmul_mx(
+                    out=z[:],
+                    lhsT=w_ord[g][:, a, 2 * P * t : 2 * P * (t + 1)].bitcast(FP4X4),
+                    lhsT_scale=ws_ord[g][:, a, P * t : P * (t + 1)],
+                    rhs=h_w[h][:, a, :].bitcast(FP4X4),
+                    rhs_scale=h_s[h][:, a, :],
+                    start=(a == 0),
+                    stop=(a == D_PASSES - 1),
+                )
+
+        def logit_sig(h, g, t):
+            soft[h, g, t] = work.tile([P, N], F32, name="soft", bufs=SOFT_BUFS)
+            nc.scalar.activation(out=soft[h, g, t][:], in_=logits[h, g, t][:], func=ACT.Sigmoid)
+
+        def logit_ln(h, g, t):
+            nc.scalar.activation(out=soft[h, g, t][:], in_=soft[h, g, t][:], func=ACT.Ln, bias=FLOOR)
+
+        def l_min(h, g, t):
+            nc.vector.tensor_tensor(
+                out=soft[h, g, t][:], in0=logits[h, g, t][:], in1=soft[h, g, t][:], op=ALU.min
+            )
+
+        def l_scale(h, g, t):
+            if (h, g) not in l16:
+                l16[h, g] = work.tile([P, SLOTS, N], BF16, name="l16")
+            col = SLOTS * g + t
+            nc.vector.tensor_scalar(
+                out=l16[h, g][:, t, :], in0=soft[h, g, t][:], scalar1=bw_pos[:, col : col + 1], scalar2=None,
+                op0=ALU.mult,
+            )
+
+        def interleave(dst, src):
+            nc.vector.tensor_copy(
+                out=dst[:].rearrange("p (c i t) -> p c t i", i=4, t=SLOTS),
+                in_=src[:].rearrange("p t (c i) -> p c t i", i=4),
+            )
+
+        def l_group(h, g):
+            grouped["l", h, g] = work.tile([P, SLOTS * N], BF16, name="l_grp", align_bytes=64)
+            interleave(grouped["l", h, g], l16[h, g])
+
+        def l_quant(h, g):
+            nc.vector.quantize_mx(out=l_q[h][g][:].bitcast(FP8X4), scales=l_s[h][g][:], in_=grouped["l", h, g][:])
+
+        sums = {}
+        y_t = {}
+        turned = {}
+        y_out = {}
+
+        def score_mm(h, v, s):
+            acc = bank()
+            sums[h, v, s] = acc
+            for g in range(B_PASSES):
+                nc.tensor.matmul_mx(
+                    out=acc[:],
+                    lhsT=c_q[g][v][:, P * s : P * (s + 1)].bitcast(FP8X4),
+                    lhsT_scale=c_s[g][v][:, P * s : P * (s + 1)],
+                    rhs=l_q[h][g][:].bitcast(FP8X4),
+                    rhs_scale=l_s[h][g][:],
+                    start=(g == 0),
+                    stop=(g == B_PASSES - 1),
+                )
+
+        def score_affine(h, v, s, on_vector):
+            if s == 0:
+                y_t[h, v] = work.tile([P, SLOTS, N], F32, name="y_t", tag="wide", bufs=WIDE_BUFS)
+            dst = y_t[h, v][:, s, :]
+            if on_vector:
+                nc.vector.tensor_scalar(
+                    out=dst, in0=sums[h, v, s][:], scalar1=scale32[:, v, s : s + 1], scalar2=bias32[:, v, s : s + 1],
+                    op0=ALU.mult, op1=ALU.add,
+                )
+            else:
+                nc.scalar.activation(
+                    out=dst, in_=sums[h, v, s][:], func=ACT.Identity,
+                    scale=scale32[:, v, s : s + 1], bias=bias32[:, v, s : s + 1],
+                )
+
+        def y_turn(h, v, j):
+            turned[h, v, j] = bank()
+            for s in range(SLOTS):
+                nc.tensor.transpose(
+                    turned[h, v, j][:, P * s : P * (s + 1)], y_t[h, v][:, s, P * j : P * (j + 1)], ident[:]
+                )
+
+        def y_drain(h, v, j, on_vector):
+            y_out[h, v, j] = work.tile([P, N], F32, name="y_out", bufs=6)
+            dst = y_out[h, v, j][:].rearrange("k (p s) -> k p s", s=SLOTS)
+            src = turned[h, v, j][:].rearrange("k (s p) -> k p s", s=SLOTS)
+            if on_vector:
+                nc.vector.tensor_copy(out=dst, in_=src)
+            else:
+                nc.scalar.copy(out=dst, in_=src)
+            rows = slice(N * h + P * j, N * h + P * (j + 1))
+            nc.sync.dma_start(out=out_0[rows, N * v : N * (v + 1)], in_=y_out[h, v, j][:])
+
+        def y_group(h, v):
+            grouped["y", h, v] = work.tile([P, SLOTS * N], BF16, name="y_grp", align_bytes=64)
+            interleave(grouped["y", h, v], y_t[h, v])
+
+        def y_quant(h, v):
+            words = work.tile([P, N], U32, name="y_words", align_bytes=64)
+            nc.vector.quantize_mx(
+                out=words[:].bitcast(FP8X4), scales=y_s[h][SLOTS * v : P, :], in_=grouped["y", h, v][:]
+            )
+            dst = out_1[v].rearrange("p m t -> p (m t)")[:, SLOTS * N * h : SLOTS * N * (h + 1)]
+            nc.sync.dma_start(out=dst.bitcast(I32), in_=words[:].bitcast(I32))
+            if v == V_GROUPS - 1:
+                for q in range(4):
+                    nc.sync.dma_start(
+                        out=out_2[:, 4 * q : 4 * q + 4, N * h : N * (h + 1)].bitcast(I32),
+                        in_=y_s[h][32 * q : 32 * q + 16, :].bitcast(I32),
+                    )
+
+        nc.vector.memset(ws_raw[0][:].bitcast(I32), 0)
+        nc.vector.memset(h_s[0][:].bitcast(I32), 0)
+        nc.vector.memset(warm_in[:], 0.0)
+        nc.vector.memset(ws_raw[1][:].bitcast(I32), 0)
+        nc.vector.memset(h_s[1][:].bitcast(I32), 0)
+        nc.vector.memset(bw_rows[:], 0.0)
+        nc.scalar.activation(out=warm_out[:], in_=warm_in[:], func=ACT.Sigmoid)
+
+        load_words(w_raw[0], w_words, 0)
+        load_scales(ws_raw[0], w_scales, 0)
+        load_words(h_w[0], h_words, 0)
+        load_scales(h_s[0], h_scales, 0, quadrants=(0, 1))
+        load_scales(h_s[0], h_scales, 0, quadrants=(2, 3), queue=nc.gpsimd)
+        load_code(0, 0)
+        load_words(w_raw[1], w_words, 1)
+        load_scales(ws_raw[1], w_scales, 1)
+        load_code(1, 0)
+        load_code(0, 1)
+        load_words(h_w[1], h_words, 1)
+        load_scales(h_s[1], h_scales, 1)
+        load_code(1, 1)
+        nc.sync.dma_start(out=scale16[:], in_=token_scale.rearrange("(v p s) -> p v s", p=P, s=SLOTS))
+        nc.sync.dma_start(out=bias16[:], in_=token_bias.rearrange("(v p s) -> p v s", p=P, s=SLOTS))
+        for g in range(B_PASSES):
+            rows = bit_weight[N * g : N * (g + 1)].rearrange("(q t r) -> t q r", t=SLOTS, r=8)
+            nc.gpsimd.dma_start(
+                out=bw_rows[SLOTS * g : SLOTS * (g + 1), :].rearrange("t (q r) -> t q r", r=8), in_=rows
+            )
+        make_identity(nc, ident[:])
+
+        order_w(0)
+
+        bw_bank = bank()
+
+        def bit_weights():
+            nc.tensor.transpose(bw_bank[:, 0:P], bw_rows32[:], ident[:])
+            nc.vector.tensor_copy(out=bw_pos[:], in_=bw_bank[:, 0 : B_PASSES * SLOTS])
+
+        units = [(g, t) for g in range(B_PASSES) for t in range(SLOTS)]
+        code_group(0, 0)
+        order_w(1)
+        nc.vector.tensor_copy(out=bw_rows32[:], in_=bw_rows[:])
+        code_quant(0, 0)
+        code_group(0, 1)
+        for i, (g, t) in enumerate(units):
+            logit_mm(0, g, t)
+            logit_sig(0, g, t)
+            if i == 4:
+                bit_weights()
+            if i == 3:
+                code_group(1, 1, on_scalar=True)
+        code_quant(0, 1)
+        code_group(1, 0)
+        code_quant(1, 1)
+        code_group(0, 2)
+        code_quant(1, 0)
+        code_group(0, 3)
+        code_quant(0, 2)
+        code_quant(0, 3)
+        for i, (g, t) in enumerate(units):
+            logit_ln(0, g, t)
+            l_min(0, g, t)
+            logit_mm(1, g, t)
+            if i > 1:
+                l_scale(0, *units[i - 2])
+        l_group(0, 0)
+        for g, t in units[-2:]:
+            l_scale(0, g, t)
+        l_quant(0, 0)
+        l_group(0, 1)
+        nc.vector.tensor_copy(out=scale32[:], in_=scale16[:])
+        nc.vector.tensor_copy(out=bias32[:], in_=bias16[:])
+        code_group(1, 2)
+        l_quant(0, 1)
+        code_quant(1, 2)
+        for i, (g, t) in enumerate(units):
+            logit_sig(1, g, t)
+        steps = [(h, v) for h in range(HALVES) for v in range(V_GROUPS)]
+        AFF_V = [(),(),(),(2,3,),(2,3,),(2,3,),(2,3,),(3,)]
+        DR_V = [(), (),(),(),(),(),(),(),(2,3,)]
+        YG = [(), (), (0,1), (2,), (3,), (4,), (5,), (), ()]
+        for i, (g, t) in enumerate(units):
+            logit_ln(1, g, t)
+            l_min(1, g, t)
+            if i < SLOTS:
+                score_mm(0, 0, i)
+        for s in range(SLOTS):
+            score_affine(0, 0, s, on_vector=False)
+        code_group(1, 3)
+        for t in range(SLOTS):
+            l_scale(1, 0, t)
+        code_quant(1, 3)
+        for i in range(1, len(steps) + 1):
+            now = steps[i] if i < len(steps) else None
+            last = steps[i - 1]
+            if now is not None:
+                for s in range(SLOTS):
+                    score_mm(*now, s)
+                    score_affine(*now, s, on_vector=(s in AFF_V[i]))
+            if i == 1:
+                l_group(1, 0)
+                for t in range(SLOTS):
+                    l_scale(1, 1, t)
+                l_quant(1, 0)
+            if i == 2:
+                l_group(1, 1)
+            if i >= len(steps) - 1:
+                y_group(*last)
+            if i == len(steps):
+                y_quant(*last)
+            for j in range(SLOTS):
+                y_turn(*last, j)
+                y_drain(*last, j, on_vector=(j in DR_V[i]))
+            if i == len(steps) - 1:
+                y_quant(*last)
+            for k in YG[i]:
+                y_group(*steps[k])
+            if i == 2:
+                l_quant(1, 1)
+            for k in YG[i]:
+                y_quant(*steps[k])

@@ -24,6 +24,9 @@ B_PASSES = B // N
 V_GROUPS = V // N
 HALVES = T // N
 SOFT_BUFS = 12
+KEEP_A = 2
+SCALE_G = True
+SAVED_BUFS = 2
 FLOOR = 2.0 ** -58
 WIDE_BUFS = 6
 CGRP_BUFS = 3
@@ -75,10 +78,10 @@ def tile_signed_bit_code_scores_k5_kernel(
             view = src[:, :, 2 * N * i : 2 * N * (i + 1)].rearrange("g p b -> p g b")
             nc.sync.dma_start(out=dst[:].bitcast(I32), in_=view.bitcast(I32))
 
-        def load_scales(dst, src, i, quadrants=range(4), queue=nc.sync):
-            for q in quadrants:
+        def load_scales(dst, src, i):
+            for q in range(4):
                 view = src[:, 4 * q : 4 * q + 4, N * i : N * (i + 1)].rearrange("g r n -> r g n")
-                queue.dma_start(out=dst[32 * q : 32 * q + 4, :, :].bitcast(I32), in_=view.bitcast(I32))
+                nc.sync.dma_start(out=dst[32 * q : 32 * q + 4, :, :].bitcast(I32), in_=view.bitcast(I32))
 
         def load_code(g, u):
             rows = code[N * g : N * (g + 1), (V // 2) * u : (V // 2) * (u + 1)]
@@ -100,8 +103,8 @@ def tile_signed_bit_code_scores_k5_kernel(
 
         def code_group(g, v, on_gpsimd=False, on_scalar=False):
             grouped["c", g, v] = work.tile([P, SLOTS * N], BF16, name="c_grp", align_bytes=64, bufs=CGRP_BUFS)
-            src = c_raw[g, v // 2][:, :, N * (v % 2) : N * (v % 2 + 1)].rearrange("p j (m s) -> p s m j", s=SLOTS)
-            dst = grouped["c", g, v][:].rearrange("p (s m j) -> p s m j", s=SLOTS, j=SLOTS)
+            src = c_raw[g, v // 2][:, :, N * (v % 2) : N * (v % 2 + 1)].rearrange("p j (m e s) -> p m s e j", e=2, s=SLOTS)
+            dst = grouped["c", g, v][:].rearrange("p (s m e j) -> p m s e j", s=SLOTS, e=2, j=SLOTS)
             if on_gpsimd:
                 nc.gpsimd.tensor_scalar(out=dst, in0=src, scalar1=1.0, scalar2=0.0, op0=ALU.mult, op1=ALU.add)
             elif on_scalar:
@@ -134,6 +137,14 @@ def tile_signed_bit_code_scores_k5_kernel(
             soft[h, g, t] = work.tile([P, N], F32, name="soft", bufs=SOFT_BUFS)
             nc.scalar.activation(out=soft[h, g, t][:], in_=logits[h, g, t][:], func=ACT.Sigmoid)
 
+        def logit_keep(h, g, t, on_vector):
+            saved = work.tile([P, N], F32, name="saved", bufs=SAVED_BUFS)
+            if on_vector:
+                nc.vector.tensor_copy(out=saved[:], in_=logits[h, g, t][:])
+            else:
+                nc.scalar.copy(out=saved[:], in_=logits[h, g, t][:])
+            logits[h, g, t] = saved
+
         def logit_ln(h, g, t):
             nc.scalar.activation(out=soft[h, g, t][:], in_=soft[h, g, t][:], func=ACT.Ln, bias=FLOOR)
 
@@ -142,13 +153,13 @@ def tile_signed_bit_code_scores_k5_kernel(
                 out=soft[h, g, t][:], in0=logits[h, g, t][:], in1=soft[h, g, t][:], op=ALU.min
             )
 
-        def l_scale(h, g, t):
+        def l_scale(h, g, t, on_gpsimd):
             if (h, g) not in l16:
                 l16[h, g] = work.tile([P, SLOTS, N], BF16, name="l16")
             col = SLOTS * g + t
-            nc.vector.tensor_scalar(
-                out=l16[h, g][:, t, :], in0=soft[h, g, t][:], scalar1=bw_pos[:, col : col + 1], scalar2=None,
-                op0=ALU.mult,
+            (nc.gpsimd if on_gpsimd else nc.vector).tensor_scalar(
+                out=l16[h, g][:, t, :], in0=soft[h, g, t][:], scalar1=bw_pos[:, col : col + 1], scalar2=0.0,
+                op0=ALU.mult, op1=ALU.add,
             )
 
         def interleave(dst, src):
@@ -227,12 +238,13 @@ def tile_signed_bit_code_scores_k5_kernel(
             )
             dst = out_1[v].rearrange("p m t -> p (m t)")[:, SLOTS * N * h : SLOTS * N * (h + 1)]
             nc.sync.dma_start(out=dst.bitcast(I32), in_=words[:].bitcast(I32))
-            if v == V_GROUPS - 1:
-                for q in range(4):
-                    nc.sync.dma_start(
-                        out=out_2[:, 4 * q : 4 * q + 4, N * h : N * (h + 1)].bitcast(I32),
-                        in_=y_s[h][32 * q : 32 * q + 16, :].bitcast(I32),
-                    )
+
+        def store_scales(h):
+            for q in range(4):
+                nc.sync.dma_start(
+                    out=out_2[:, 4 * q : 4 * q + 4, N * h : N * (h + 1)].bitcast(I32),
+                    in_=y_s[h][32 * q : 32 * q + 16, :].bitcast(I32),
+                )
 
         nc.vector.memset(ws_raw[0][:].bitcast(I32), 0)
         nc.vector.memset(h_s[0][:].bitcast(I32), 0)
@@ -245,11 +257,15 @@ def tile_signed_bit_code_scores_k5_kernel(
         load_words(w_raw[0], w_words, 0)
         load_scales(ws_raw[0], w_scales, 0)
         load_words(h_w[0], h_words, 0)
-        load_scales(h_s[0], h_scales, 0, quadrants=(0, 1))
-        load_scales(h_s[0], h_scales, 0, quadrants=(2, 3), queue=nc.gpsimd)
+        load_scales(h_s[0], h_scales, 0)
         load_code(0, 0)
         load_words(w_raw[1], w_words, 1)
         load_scales(ws_raw[1], w_scales, 1)
+        for g in range(B_PASSES):
+            rows = bit_weight[N * g : N * (g + 1)].rearrange("(q t r) -> t q r", t=SLOTS, r=8)
+            nc.sync.dma_start(
+                out=bw_rows[SLOTS * g : SLOTS * (g + 1), :].rearrange("t (q r) -> t q r", r=8), in_=rows
+            )
         load_code(1, 0)
         load_code(0, 1)
         load_words(h_w[1], h_words, 1)
@@ -257,11 +273,6 @@ def tile_signed_bit_code_scores_k5_kernel(
         load_code(1, 1)
         nc.sync.dma_start(out=scale16[:], in_=token_scale.rearrange("(v p s) -> p v s", p=P, s=SLOTS))
         nc.sync.dma_start(out=bias16[:], in_=token_bias.rearrange("(v p s) -> p v s", p=P, s=SLOTS))
-        for g in range(B_PASSES):
-            rows = bit_weight[N * g : N * (g + 1)].rearrange("(q t r) -> t q r", t=SLOTS, r=8)
-            nc.gpsimd.dma_start(
-                out=bw_rows[SLOTS * g : SLOTS * (g + 1), :].rearrange("t (q r) -> t q r", r=8), in_=rows
-            )
         make_identity(nc, ident[:])
 
         order_w(0)
@@ -275,83 +286,101 @@ def tile_signed_bit_code_scores_k5_kernel(
         units = [(g, t) for g in range(B_PASSES) for t in range(SLOTS)]
         code_group(0, 0)
         order_w(1)
-        nc.vector.tensor_copy(out=bw_rows32[:], in_=bw_rows[:])
         code_quant(0, 0)
         code_group(0, 1)
+        nc.vector.tensor_copy(out=bw_rows32[:], in_=bw_rows[:])
         for i, (g, t) in enumerate(units):
             logit_mm(0, g, t)
             logit_sig(0, g, t)
-            if i == 4:
-                bit_weights()
+            if i < KEEP_A:
+                logit_keep(0, g, t, on_vector=False)
             if i == 3:
                 code_group(1, 1, on_scalar=True)
-        code_quant(0, 1)
-        code_group(1, 0)
-        code_quant(1, 1)
+                code_quant(0, 1)
+                code_group(1, 0)
+            if i == 5:
+                code_quant(1, 0)
+                bit_weights()
         code_group(0, 2)
-        code_quant(1, 0)
+        code_quant(1, 1)
         code_group(0, 3)
         code_quant(0, 2)
         code_quant(0, 3)
-        for i, (g, t) in enumerate(units):
+        for g, t in units[:KEEP_A]:
+            logit_mm(1, g, t)
+        for i, (g, t) in enumerate(units[KEEP_A:]):
             logit_ln(0, g, t)
             l_min(0, g, t)
+            l_scale(0, g, t, SCALE_G)
             logit_mm(1, g, t)
-            if i > 1:
-                l_scale(0, *units[i - 2])
-        l_group(0, 0)
-        for g, t in units[-2:]:
-            l_scale(0, g, t)
-        l_quant(0, 0)
-        l_group(0, 1)
+        for g, t in units[:KEEP_A]:
+            logit_ln(0, g, t)
+            l_min(0, g, t)
         nc.vector.tensor_copy(out=scale32[:], in_=scale16[:])
         nc.vector.tensor_copy(out=bias32[:], in_=bias16[:])
-        code_group(1, 2)
+        for g, t in units[:KEEP_A]:
+            l_scale(0, g, t, False)
+        l_group(0, 1)
+        l_group(0, 0)
         l_quant(0, 1)
-        code_quant(1, 2)
+        l_quant(0, 0)
+        code_group(1, 2)
+        code_group(1, 3)
         for i, (g, t) in enumerate(units):
             logit_sig(1, g, t)
         steps = [(h, v) for h in range(HALVES) for v in range(V_GROUPS)]
-        AFF_V = [(),(),(),(2,3,),(2,3,),(2,3,),(2,3,),(3,)]
-        DR_V = [(), (),(),(),(),(),(),(),(2,3,)]
-        YG = [(), (), (0,1), (2,), (3,), (4,), (5,), (), ()]
+        AFF_V = [(),(),(),(3,)]+[(2,3)]*3+[(0,1,2,3)]
+        DR_V = [()]*9
         for i, (g, t) in enumerate(units):
             logit_ln(1, g, t)
             l_min(1, g, t)
+            if i < len(units) - 1:
+                l_scale(1, g, t, SCALE_G)
             if i < SLOTS:
                 score_mm(0, 0, i)
         for s in range(SLOTS):
             score_affine(0, 0, s, on_vector=False)
-        code_group(1, 3)
-        for t in range(SLOTS):
-            l_scale(1, 0, t)
+        l_scale(1, 1, 3, False)
+        code_quant(1, 2)
+        l_group(1, 0)
         code_quant(1, 3)
-        for i in range(1, len(steps) + 1):
-            now = steps[i] if i < len(steps) else None
+        y_group(0, 0)
+        l_quant(1, 0)
+        for i in range(1, len(steps) - 1):
+            now = steps[i]
             last = steps[i - 1]
-            if now is not None:
-                for s in range(SLOTS):
-                    score_mm(*now, s)
-                    score_affine(*now, s, on_vector=(s in AFF_V[i]))
+            y_quant(*last)
+            if last == (0, V_GROUPS - 1):
+                store_scales(0)
+            for s in range(SLOTS):
+                score_mm(*now, s)
+                score_affine(*now, s, on_vector=(s in AFF_V[i]))
             if i == 1:
-                l_group(1, 0)
-                for t in range(SLOTS):
-                    l_scale(1, 1, t)
-                l_quant(1, 0)
-            if i == 2:
                 l_group(1, 1)
-            if i >= len(steps) - 1:
-                y_group(*last)
-            if i == len(steps):
-                y_quant(*last)
+            y_group(*now)
+            if i == 1:
+                l_quant(1, 1)
             for j in range(SLOTS):
                 y_turn(*last, j)
                 y_drain(*last, j, on_vector=(j in DR_V[i]))
-            if i == len(steps) - 1:
-                y_quant(*last)
-            for k in YG[i]:
-                y_group(*steps[k])
-            if i == 2:
-                l_quant(1, 1)
-            for k in YG[i]:
-                y_quant(*steps[k])
+        last, now = steps[-2], steps[-1]
+        y_quant(*last)
+        for pair in ((0, 1), (2, 3)):
+            for j in pair:
+                y_turn(*last, j)
+            for s in pair:
+                score_mm(*now, s)
+            for j in pair:
+                y_drain(*last, j, on_vector=False)
+            for s in pair:
+                score_affine(*now, s, on_vector=(s in AFF_V[7]))
+        y_group(*now)
+        for j in range(2):
+            y_turn(*now, j)
+            y_drain(*now, j, on_vector=False)
+        y_quant(*now)
+        y_turn(*now, 2)
+        y_drain(*now, 2, on_vector=False)
+        y_turn(*now, 3)
+        y_drain(*now, 3, on_vector=True)
+        store_scales(1)

@@ -29,7 +29,7 @@ SCALE_G = True
 SAVED_BUFS = 2
 FLOOR = 2.0 ** -58
 WIDE_BUFS = 6
-CGRP_BUFS = 3
+CGRP_BUFS = 4
 
 
 def tile_signed_bit_code_scores_k5_kernel(
@@ -164,8 +164,8 @@ def tile_signed_bit_code_scores_k5_kernel(
 
         def interleave(dst, src):
             nc.vector.tensor_copy(
-                out=dst[:].rearrange("p (c i t) -> p c t i", i=4, t=SLOTS),
-                in_=src[:].rearrange("p t (c i) -> p c t i", i=4),
+                out=dst[:].rearrange("p (c t) -> p c t", t=SLOTS),
+                in_=src[:].rearrange("p t c -> p c t"),
             )
 
         def l_group(h, g):
@@ -179,6 +179,7 @@ def tile_signed_bit_code_scores_k5_kernel(
         y_t = {}
         turned = {}
         y_out = {}
+        y_words = {}
 
         def score_mm(h, v, s):
             acc = bank()
@@ -217,7 +218,7 @@ def tile_signed_bit_code_scores_k5_kernel(
                 )
 
         def y_drain(h, v, j, on_vector):
-            y_out[h, v, j] = work.tile([P, N], F32, name="y_out", bufs=6)
+            y_out[h, v, j] = work.tile([P, N], F32, name="y_out", bufs=10)
             dst = y_out[h, v, j][:].rearrange("k (p s) -> k p s", s=SLOTS)
             src = turned[h, v, j][:].rearrange("k (s p) -> k p s", s=SLOTS)
             if on_vector:
@@ -232,10 +233,14 @@ def tile_signed_bit_code_scores_k5_kernel(
             interleave(grouped["y", h, v], y_t[h, v])
 
         def y_quant(h, v):
-            words = work.tile([P, N], U32, name="y_words", align_bytes=64)
+            words = work.tile([P, N], U32, name="y_words", align_bytes=64, bufs=3)
+            y_words[h, v] = words
             nc.vector.quantize_mx(
                 out=words[:].bitcast(FP8X4), scales=y_s[h][SLOTS * v : P, :], in_=grouped["y", h, v][:]
             )
+
+        def store_words(h, v):
+            words = y_words[h, v]
             dst = out_1[v].rearrange("p m t -> p (m t)")[:, SLOTS * N * h : SLOTS * N * (h + 1)]
             nc.sync.dma_start(out=dst.bitcast(I32), in_=words[:].bitcast(I32))
 
@@ -287,7 +292,6 @@ def tile_signed_bit_code_scores_k5_kernel(
         code_group(0, 0)
         order_w(1)
         code_quant(0, 0)
-        code_group(0, 1)
         nc.vector.tensor_copy(out=bw_rows32[:], in_=bw_rows[:])
         for i, (g, t) in enumerate(units):
             logit_mm(0, g, t)
@@ -295,41 +299,41 @@ def tile_signed_bit_code_scores_k5_kernel(
             if i < KEEP_A:
                 logit_keep(0, g, t, on_vector=False)
             if i == 3:
-                code_group(1, 1, on_scalar=True)
-                code_quant(0, 1)
-                code_group(1, 0)
-            if i == 5:
-                code_quant(1, 0)
                 bit_weights()
-        code_group(0, 2)
+                code_group(0, 1, on_scalar=True)
+        code_group(1, 0)
+        code_group(1, 1)
+        code_quant(1, 0)
         code_quant(1, 1)
+        code_group(0, 2)
+        code_quant(0, 1)
         code_group(0, 3)
         code_quant(0, 2)
-        code_quant(0, 3)
         for g, t in units[:KEEP_A]:
             logit_mm(1, g, t)
         for i, (g, t) in enumerate(units[KEEP_A:]):
             logit_ln(0, g, t)
             l_min(0, g, t)
-            l_scale(0, g, t, SCALE_G)
+            if (g, t) != units[-1]:
+                l_scale(0, g, t, SCALE_G)
             logit_mm(1, g, t)
         for g, t in units[:KEEP_A]:
             logit_ln(0, g, t)
             l_min(0, g, t)
         nc.vector.tensor_copy(out=scale32[:], in_=scale16[:])
         nc.vector.tensor_copy(out=bias32[:], in_=bias16[:])
-        for g, t in units[:KEEP_A]:
+        for g, t in units[-1:] + units[:KEEP_A]:
             l_scale(0, g, t, False)
+        code_quant(0, 3)
         l_group(0, 1)
         l_group(0, 0)
         l_quant(0, 1)
         l_quant(0, 0)
         code_group(1, 2)
-        code_group(1, 3)
         for i, (g, t) in enumerate(units):
             logit_sig(1, g, t)
         steps = [(h, v) for h in range(HALVES) for v in range(V_GROUPS)]
-        AFF_V = [(),(),(),(3,)]+[(2,3)]*3+[(0,1,2,3)]
+        AFF_V = [(),(),()]+[(2,3)]*4+[(0,1,2,3)]
         DR_V = [()]*9
         for i, (g, t) in enumerate(units):
             logit_ln(1, g, t)
@@ -342,6 +346,7 @@ def tile_signed_bit_code_scores_k5_kernel(
             score_affine(0, 0, s, on_vector=False)
         l_scale(1, 1, 3, False)
         code_quant(1, 2)
+        code_group(1, 3)
         l_group(1, 0)
         code_quant(1, 3)
         y_group(0, 0)
@@ -349,12 +354,10 @@ def tile_signed_bit_code_scores_k5_kernel(
         for i in range(1, len(steps) - 1):
             now = steps[i]
             last = steps[i - 1]
-            y_quant(*last)
-            if last == (0, V_GROUPS - 1):
-                store_scales(0)
             for s in range(SLOTS):
                 score_mm(*now, s)
                 score_affine(*now, s, on_vector=(s in AFF_V[i]))
+            y_quant(*last)
             if i == 1:
                 l_group(1, 1)
             y_group(*now)
@@ -363,8 +366,10 @@ def tile_signed_bit_code_scores_k5_kernel(
             for j in range(SLOTS):
                 y_turn(*last, j)
                 y_drain(*last, j, on_vector=(j in DR_V[i]))
+            store_words(*last)
+            if last == (0, V_GROUPS - 1):
+                store_scales(0)
         last, now = steps[-2], steps[-1]
-        y_quant(*last)
         for pair in ((0, 1), (2, 3)):
             for j in pair:
                 y_turn(*last, j)
@@ -374,6 +379,9 @@ def tile_signed_bit_code_scores_k5_kernel(
                 y_drain(*last, j, on_vector=False)
             for s in pair:
                 score_affine(*now, s, on_vector=(s in AFF_V[7]))
+            if pair[0] == 0:
+                y_quant(*last)
+                store_words(*last)
         y_group(*now)
         for j in range(2):
             y_turn(*now, j)
@@ -381,6 +389,7 @@ def tile_signed_bit_code_scores_k5_kernel(
         y_quant(*now)
         y_turn(*now, 2)
         y_drain(*now, 2, on_vector=False)
+        store_words(*now)
         y_turn(*now, 3)
         y_drain(*now, 3, on_vector=True)
         store_scales(1)

@@ -26,6 +26,9 @@ HALVES = T // N
 SOFT_BUFS = 12
 KEEP_A = 2
 SCALE_G = True
+SHARED = 320
+WARM = 3
+FIRST_SHARED = 3
 SAVED_BUFS = 2
 FLOOR = 2.0 ** -58
 WIDE_BUFS = 6
@@ -83,34 +86,42 @@ def tile_signed_bit_code_scores_k5_kernel(
                 view = src[:, 4 * q : 4 * q + 4, N * i : N * (i + 1)].rearrange("g r n -> r g n")
                 nc.sync.dma_start(out=dst[32 * q : 32 * q + 4, :, :].bitcast(I32), in_=view.bitcast(I32))
 
-        def load_code(g, u):
-            rows = code[N * g : N * (g + 1), (V // 2) * u : (V // 2) * (u + 1)]
+        def load_code(g, u, cols=slice(0, V // 2)):
+            rows = code[N * g : N * (g + 1), (V // 2) * u + cols.start : (V // 2) * u + cols.stop]
             rows = rows.rearrange("(q t r) v -> t q r v", t=SLOTS, r=8)
             for t in range(SLOTS):
-                nc.sync.dma_start(out=c_raw[g, u][:, t, :], in_=rows[t])
+                nc.sync.dma_start(out=c_raw[g, u][:, t, cols], in_=rows[t])
 
-        def order_w(g):
+        def order_scales(g):
             nc.vector.tensor_copy(
                 out=ws_ord[g][:].bitcast(I32).rearrange("p a (t q w) -> p a t q w", t=SLOTS, q=16),
                 in_=ws_raw[g][:].bitcast(I32).rearrange("p a (q t w) -> p a t q w", t=SLOTS, q=16),
             )
+
+        def order_words(g, slots):
             nc.vector.tensor_copy(
-                out=w_ord[g][:].bitcast(I32).rearrange("p a (t q w) -> p a t q w", t=SLOTS, q=16),
-                in_=w_raw[g][:].bitcast(I32).rearrange("p a (q t w) -> p a t q w", t=SLOTS, q=16),
+                out=w_ord[g][:].bitcast(I32).rearrange("p a (t q w) -> p a t q w", t=SLOTS, q=16)[:, :, slots],
+                in_=w_raw[g][:].bitcast(I32).rearrange("p a (q t w) -> p a t q w", t=SLOTS, q=16)[:, :, slots],
             )
 
         grouped = {}
 
-        def code_group(g, v, on_gpsimd=False, on_scalar=False):
-            grouped["c", g, v] = work.tile([P, SLOTS * N], BF16, name="c_grp", align_bytes=64, bufs=CGRP_BUFS)
-            src = c_raw[g, v // 2][:, :, N * (v % 2) : N * (v % 2 + 1)].rearrange("p j (m e s) -> p m s e j", e=2, s=SLOTS)
+        def code_views(g, v):
+            src = c_raw[g, v // 2][:, :, N * (v % 2) : N * (v % 2 + 1)]
+            src = src.rearrange("p j (m e s) -> p m s e j", e=2, s=SLOTS)
             dst = grouped["c", g, v][:].rearrange("p (s m e j) -> p m s e j", s=SLOTS, e=2, j=SLOTS)
-            if on_gpsimd:
-                nc.gpsimd.tensor_scalar(out=dst, in0=src, scalar1=1.0, scalar2=0.0, op0=ALU.mult, op1=ALU.add)
-            elif on_scalar:
-                nc.scalar.copy(out=dst, in_=src)
-            else:
-                nc.vector.tensor_copy(out=dst, in_=src)
+            return dst, src
+
+        def code_group(g, v):
+            grouped["c", g, v] = work.tile([P, SLOTS * N], BF16, name="c_grp", align_bytes=64, bufs=CGRP_BUFS)
+            dst, src = code_views(g, v)
+            nc.vector.tensor_copy(out=dst, in_=src)
+
+        def code_group_on_scalar(g, v, part):
+            if part == 0:
+                grouped["c", g, v] = work.tile([P, SLOTS * N], BF16, name="c_grp", align_bytes=64, bufs=CGRP_BUFS)
+            dst, src = code_views(g, v)
+            nc.scalar.copy(out=dst[:, 32 * part : 32 * (part + 1)], in_=src[:, 32 * part : 32 * (part + 1)])
 
         def code_quant(g, v):
             nc.vector.quantize_mx(out=c_q[g][v][:].bitcast(FP8X4), scales=c_s[g][v][:], in_=grouped["c", g, v][:])
@@ -162,15 +173,15 @@ def tile_signed_bit_code_scores_k5_kernel(
                 op0=ALU.mult, op1=ALU.add,
             )
 
-        def interleave(dst, src):
+        def interleave(dst, src, cols):
             nc.vector.tensor_copy(
-                out=dst[:].rearrange("p (c t) -> p c t", t=SLOTS),
-                in_=src[:].rearrange("p t c -> p c t"),
+                out=dst[:, SLOTS * cols.start : SLOTS * cols.stop].rearrange("p (c i t) -> p c t i", i=4, t=SLOTS),
+                in_=src[:, :, cols].rearrange("p t (c i) -> p c t i", i=4),
             )
 
         def l_group(h, g):
             grouped["l", h, g] = work.tile([P, SLOTS * N], BF16, name="l_grp", align_bytes=64)
-            interleave(grouped["l", h, g], l16[h, g])
+            interleave(grouped["l", h, g], l16[h, g], slice(0, N))
 
         def l_quant(h, g):
             nc.vector.quantize_mx(out=l_q[h][g][:].bitcast(FP8X4), scales=l_s[h][g][:], in_=grouped["l", h, g][:])
@@ -228,9 +239,19 @@ def tile_signed_bit_code_scores_k5_kernel(
             rows = slice(N * h + P * j, N * h + P * (j + 1))
             nc.sync.dma_start(out=out_0[rows, N * v : N * (v + 1)], in_=y_out[h, v, j][:])
 
-        def y_group(h, v):
-            grouped["y", h, v] = work.tile([P, SLOTS * N], BF16, name="y_grp", align_bytes=64)
-            interleave(grouped["y", h, v], y_t[h, v])
+        def y_group_shared(h, v):
+            grouped["y", h, v] = work.tile([P, SLOTS * N], BF16, name="y_grp", align_bytes=64, bufs=3)
+            nc.gpsimd.tensor_scalar(
+                out=grouped["y", h, v][:, 0 : SLOTS * SHARED].rearrange("p (c t) -> p c t", t=SLOTS),
+                in0=y_t[h, v][:, :, 0:SHARED].rearrange("p t c -> p c t"),
+                scalar1=1.0, scalar2=0.0, op0=ALU.mult, op1=ALU.add,
+            )
+
+        def y_group(h, v, first=0):
+            if first == 0:
+                grouped["y", h, v] = work.tile([P, SLOTS * N], BF16, name="y_grp", align_bytes=64, bufs=3)
+            if first < N:
+                interleave(grouped["y", h, v], y_t[h, v], slice(first, N))
 
         def y_quant(h, v):
             words = work.tile([P, N], U32, name="y_words", align_bytes=64, bufs=3)
@@ -263,15 +284,17 @@ def tile_signed_bit_code_scores_k5_kernel(
         load_scales(ws_raw[0], w_scales, 0)
         load_words(h_w[0], h_words, 0)
         load_scales(h_s[0], h_scales, 0)
-        load_code(0, 0)
+        load_code(0, 0, slice(0, N))
         load_words(w_raw[1], w_words, 1)
         load_scales(ws_raw[1], w_scales, 1)
+        load_code(1, 0, slice(0, N))
+        load_code(0, 0, slice(N, 2 * N))
         for g in range(B_PASSES):
             rows = bit_weight[N * g : N * (g + 1)].rearrange("(q t r) -> t q r", t=SLOTS, r=8)
             nc.sync.dma_start(
                 out=bw_rows[SLOTS * g : SLOTS * (g + 1), :].rearrange("t (q r) -> t q r", r=8), in_=rows
             )
-        load_code(1, 0)
+        load_code(1, 0, slice(N, 2 * N))
         load_code(0, 1)
         load_words(h_w[1], h_words, 1)
         load_scales(h_s[1], h_scales, 1)
@@ -280,9 +303,21 @@ def tile_signed_bit_code_scores_k5_kernel(
         nc.sync.dma_start(out=bias16[:], in_=token_bias.rearrange("(v p s) -> p v s", p=P, s=SLOTS))
         make_identity(nc, ident[:])
 
-        order_w(0)
+        order_words(0, slice(0, 2))
+        order_scales(0)
+        order_words(0, slice(2, SLOTS))
 
         bw_bank = bank()
+        for a in range(WARM):
+            nc.tensor.matmul_mx(
+                out=bw_bank[:],
+                lhsT=w_raw[0][:, a, 0 : 2 * P].bitcast(FP4X4),
+                lhsT_scale=ws_raw[0][:, a, 0:P],
+                rhs=w_raw[0][:, a, :].bitcast(FP4X4),
+                rhs_scale=ws_raw[0][:, a, :],
+                start=True,
+                stop=True,
+            )
 
         def bit_weights():
             nc.tensor.transpose(bw_bank[:, 0:P], bw_rows32[:], ident[:])
@@ -290,25 +325,28 @@ def tile_signed_bit_code_scores_k5_kernel(
 
         units = [(g, t) for g in range(B_PASSES) for t in range(SLOTS)]
         code_group(0, 0)
-        order_w(1)
+        order_words(1, slice(0, SLOTS))
         code_quant(0, 0)
+        order_scales(1)
+        code_group(1, 0)
         nc.vector.tensor_copy(out=bw_rows32[:], in_=bw_rows[:])
+        code_quant(1, 0)
         for i, (g, t) in enumerate(units):
             logit_mm(0, g, t)
             logit_sig(0, g, t)
             if i < KEEP_A:
                 logit_keep(0, g, t, on_vector=False)
-            if i == 3:
+            if i == 4:
                 bit_weights()
-                code_group(0, 1, on_scalar=True)
-        code_group(1, 0)
+            if i in (3, 5):
+                code_group_on_scalar(0, 1, (i - 3) // 2)
         code_group(1, 1)
-        code_quant(1, 0)
-        code_quant(1, 1)
         code_group(0, 2)
-        code_quant(0, 1)
+        code_quant(1, 1)
         code_group(0, 3)
+        code_quant(0, 1)
         code_quant(0, 2)
+        code_quant(0, 3)
         for g, t in units[:KEEP_A]:
             logit_mm(1, g, t)
         for i, (g, t) in enumerate(units[KEEP_A:]):
@@ -324,17 +362,17 @@ def tile_signed_bit_code_scores_k5_kernel(
         nc.vector.tensor_copy(out=bias32[:], in_=bias16[:])
         for g, t in units[-1:] + units[:KEEP_A]:
             l_scale(0, g, t, False)
-        code_quant(0, 3)
         l_group(0, 1)
         l_group(0, 0)
         l_quant(0, 1)
         l_quant(0, 0)
         code_group(1, 2)
+        code_group(1, 3)
         for i, (g, t) in enumerate(units):
             logit_sig(1, g, t)
         steps = [(h, v) for h in range(HALVES) for v in range(V_GROUPS)]
-        AFF_V = [(),(),()]+[(2,3)]*4+[(0,1,2,3)]
-        DR_V = [()]*9
+        AFF_V = (1,2,3)
+        DR_V = (0,1,2)
         for i, (g, t) in enumerate(units):
             logit_ln(1, g, t)
             l_min(1, g, t)
@@ -346,7 +384,6 @@ def tile_signed_bit_code_scores_k5_kernel(
             score_affine(0, 0, s, on_vector=False)
         l_scale(1, 1, 3, False)
         code_quant(1, 2)
-        code_group(1, 3)
         l_group(1, 0)
         code_quant(1, 3)
         y_group(0, 0)
@@ -356,18 +393,27 @@ def tile_signed_bit_code_scores_k5_kernel(
             last = steps[i - 1]
             for s in range(SLOTS):
                 score_mm(*now, s)
-                score_affine(*now, s, on_vector=(s in AFF_V[i]))
-            y_quant(*last)
+                score_affine(*now, s, on_vector=False)
+            if i <= FIRST_SHARED:
+                y_quant(*last)
             if i == 1:
                 l_group(1, 1)
-            y_group(*now)
+            if i < FIRST_SHARED:
+                y_group(*now)
+            else:
+                y_group_shared(*now)
             if i == 1:
                 l_quant(1, 1)
             for j in range(SLOTS):
                 y_turn(*last, j)
-                y_drain(*last, j, on_vector=(j in DR_V[i]))
-            store_words(*last)
-            if last == (0, V_GROUPS - 1):
+                y_drain(*last, j, on_vector=(i >= FIRST_SHARED and j in DR_V))
+            if i <= FIRST_SHARED:
+                store_words(*last)
+            if i >= FIRST_SHARED:
+                y_group(*now, SHARED)
+                y_quant(*now)
+                store_words(*now)
+            if now == (0, V_GROUPS - 1):
                 store_scales(0)
         last, now = steps[-2], steps[-1]
         for pair in ((0, 1), (2, 3)):
@@ -378,10 +424,7 @@ def tile_signed_bit_code_scores_k5_kernel(
             for j in pair:
                 y_drain(*last, j, on_vector=False)
             for s in pair:
-                score_affine(*now, s, on_vector=(s in AFF_V[7]))
-            if pair[0] == 0:
-                y_quant(*last)
-                store_words(*last)
+                score_affine(*now, s, on_vector=(s in AFF_V))
         y_group(*now)
         for j in range(2):
             y_turn(*now, j)

@@ -19,20 +19,27 @@ ALU = mybir.AluOpType
 P = 128
 N = 512
 SLOTS = 4
+BLOCKS = 16
+RUN = 8
+QUADRANTS = 4
 D_PASSES = D // N
-B_PASSES = B // N
-V_GROUPS = V // N
+BIT_GROUPS = B // N
+TOKEN_GROUPS = V // N
 HALVES = T // N
+BANKS = 8
+
+FLOOR = 2.0**-58
+WARM_PASSES = 3
+SAVED_BANKS = 2
+GPSIMD_COLUMNS = 320
+FIRST_SHARED_STEP = 3
+VECTOR_DRAINS = 3
+
 SOFT_BUFS = 12
-KEEP_A = 2
-SCALE_G = True
-SHARED = 320
-WARM = 3
-FIRST_SHARED = 3
-SAVED_BUFS = 2
-FLOOR = 2.0 ** -58
+CODE_GROUP_BUFS = 4
 WIDE_BUFS = 6
-CGRP_BUFS = 4
+Y_OUT_BUFS = 10
+Y_PLANE_BUFS = 3
 
 
 def tile_signed_bit_code_scores_k5_kernel(
@@ -42,7 +49,7 @@ def tile_signed_bit_code_scores_k5_kernel(
     with ExitStack() as ctx:
         keep = ctx.enter_context(tc.tile_pool(name="keep", bufs=1))
         work = ctx.enter_context(tc.tile_pool(name="work", bufs=2))
-        psum = ctx.enter_context(tc.psum_pool(name="psum", bufs=8))
+        psum = ctx.enter_context(tc.psum_pool(name="psum", bufs=BANKS))
         ctx.enter_context(tc.manual_schedule())
 
         def kept(name, shape, dtype):
@@ -51,91 +58,85 @@ def tile_signed_bit_code_scores_k5_kernel(
         def bank():
             return psum.tile([P, N], F32, name="bank")
 
-        w_raw = [kept("w_raw%d" % g, [P, D_PASSES, 2 * N], U8) for g in range(B_PASSES)]
-        ws_raw = [kept("ws_raw%d" % g, [P, D_PASSES, N], U8) for g in range(B_PASSES)]
-        w_ord = [kept("w_ord%d" % g, [P, D_PASSES, 2 * N], U8) for g in range(B_PASSES)]
-        ws_ord = [kept("ws_ord%d" % g, [P, D_PASSES, N], U8) for g in range(B_PASSES)]
+        w_raw = [kept("w_raw%d" % g, [P, D_PASSES, 2 * N], U8) for g in range(BIT_GROUPS)]
+        ws_raw = [kept("ws_raw%d" % g, [P, D_PASSES, N], U8) for g in range(BIT_GROUPS)]
+        w_ord = [kept("w_ord%d" % g, [P, D_PASSES, 2 * N], U8) for g in range(BIT_GROUPS)]
+        ws_ord = [kept("ws_ord%d" % g, [P, D_PASSES, N], U8) for g in range(BIT_GROUPS)]
         h_w = [kept("h_w%d" % h, [P, D_PASSES, 2 * N], U8) for h in range(HALVES)]
         h_s = [kept("h_s%d" % h, [P, D_PASSES, N], U8) for h in range(HALVES)]
         c_raw = {}
-        for u in range(2):
-            for g in range(B_PASSES):
-                c_raw[g, u] = work.tile([P, SLOTS, V // 2], BF16, name="c_raw", tag="wide", bufs=WIDE_BUFS)
-        c_q = [[kept("c_q%d_%d" % (g, v), [P, N], U32) for v in range(V_GROUPS)] for g in range(B_PASSES)]
-        c_s = [[kept("c_s%d_%d" % (g, v), [P, N], U8) for v in range(V_GROUPS)] for g in range(B_PASSES)]
-        l_q = [[kept("l_q%d_%d" % (h, g), [P, N], U32) for g in range(B_PASSES)] for h in range(HALVES)]
-        l_s = [[kept("l_s%d_%d" % (h, g), [P, N], U8) for g in range(B_PASSES)] for h in range(HALVES)]
+        for g in range(BIT_GROUPS):
+            for v in range(2):
+                c_raw[g, v] = kept("c_raw%d_%d" % (g, v), [P, SLOTS, N], BF16)
+            late = work.tile([P, SLOTS, 2 * N], BF16, name="c_late", tag="wide", bufs=WIDE_BUFS)
+            c_raw[g, 2, 3] = late
+            c_raw[g, 2] = late[:, :, 0:N]
+            c_raw[g, 3] = late[:, :, N : 2 * N]
+        c_q = [[kept("c_q%d_%d" % (g, v), [P, N], U32) for v in range(TOKEN_GROUPS)] for g in range(BIT_GROUPS)]
+        c_s = [[kept("c_s%d_%d" % (g, v), [P, N], U8) for v in range(TOKEN_GROUPS)] for g in range(BIT_GROUPS)]
+        l_q = [[kept("l_q%d_%d" % (h, g), [P, N], U32) for g in range(BIT_GROUPS)] for h in range(HALVES)]
+        l_s = [[kept("l_s%d_%d" % (h, g), [P, N], U8) for g in range(BIT_GROUPS)] for h in range(HALVES)]
         y_s = [kept("y_s%d" % h, [P, N], U8) for h in range(HALVES)]
         ident = kept("ident", [P, P], F32)
         bw_rows = kept("bw_rows", [P, P], BF16)
         bw_rows32 = kept("bw_rows32", [P, P], F32)
-        bw_pos = kept("bw_pos", [P, B_PASSES * SLOTS], F32)
-        scale16 = kept("scale16", [P, V_GROUPS, SLOTS], BF16)
-        bias16 = kept("bias16", [P, V_GROUPS, SLOTS], BF16)
-        scale32 = kept("scale32", [P, V_GROUPS, SLOTS], F32)
-        bias32 = kept("bias32", [P, V_GROUPS, SLOTS], F32)
+        bw_cols = kept("bw_cols", [P, BIT_GROUPS * SLOTS], F32)
+        scale16 = kept("scale16", [P, TOKEN_GROUPS, SLOTS], BF16)
+        bias16 = kept("bias16", [P, TOKEN_GROUPS, SLOTS], BF16)
+        scale32 = kept("scale32", [P, TOKEN_GROUPS, SLOTS], F32)
+        bias32 = kept("bias32", [P, TOKEN_GROUPS, SLOTS], F32)
         warm_in = kept("warm_in", [P, 1], F32)
         warm_out = kept("warm_out", [P, 1], F32)
 
-        def load_words(dst, src, i):
-            view = src[:, :, 2 * N * i : 2 * N * (i + 1)].rearrange("g p b -> p g b")
+        def load_words(dst, src, part):
+            view = src[:, :, 2 * N * part : 2 * N * (part + 1)].rearrange("a p c -> p a c")
             nc.sync.dma_start(out=dst[:].bitcast(I32), in_=view.bitcast(I32))
 
-        def load_scales(dst, src, i):
-            for q in range(4):
-                view = src[:, 4 * q : 4 * q + 4, N * i : N * (i + 1)].rearrange("g r n -> r g n")
+        def load_scales(dst, src, part):
+            for q in range(QUADRANTS):
+                view = src[:, 4 * q : 4 * q + 4, N * part : N * (part + 1)].rearrange("a r c -> r a c")
                 nc.sync.dma_start(out=dst[32 * q : 32 * q + 4, :, :].bitcast(I32), in_=view.bitcast(I32))
 
-        def load_code(g, u, cols=slice(0, V // 2)):
-            rows = code[N * g : N * (g + 1), (V // 2) * u + cols.start : (V // 2) * u + cols.stop]
-            rows = rows.rearrange("(q t r) v -> t q r v", t=SLOTS, r=8)
+        def load_code(g, *token_groups):
+            rows = code[N * g : N * (g + 1), N * token_groups[0] : N * (token_groups[-1] + 1)]
+            rows = rows.rearrange("(b t r) c -> t b r c", t=SLOTS, r=RUN)
             for t in range(SLOTS):
-                nc.sync.dma_start(out=c_raw[g, u][:, t, cols], in_=rows[t])
+                nc.sync.dma_start(out=c_raw[(g, *token_groups)][:, t, :], in_=rows[t])
 
         def order_scales(g):
             nc.vector.tensor_copy(
-                out=ws_ord[g][:].bitcast(I32).rearrange("p a (t q w) -> p a t q w", t=SLOTS, q=16),
-                in_=ws_raw[g][:].bitcast(I32).rearrange("p a (q t w) -> p a t q w", t=SLOTS, q=16),
+                out=ws_ord[g][:].bitcast(I32).rearrange("p a (t b w) -> p a t b w", t=SLOTS, b=BLOCKS),
+                in_=ws_raw[g][:].bitcast(I32).rearrange("p a (b t w) -> p a t b w", t=SLOTS, b=BLOCKS),
             )
 
         def order_words(g, slots):
             nc.vector.tensor_copy(
-                out=w_ord[g][:].bitcast(I32).rearrange("p a (t q w) -> p a t q w", t=SLOTS, q=16)[:, :, slots],
-                in_=w_raw[g][:].bitcast(I32).rearrange("p a (q t w) -> p a t q w", t=SLOTS, q=16)[:, :, slots],
+                out=w_ord[g][:].bitcast(I32).rearrange("p a (t b w) -> p a t b w", t=SLOTS, b=BLOCKS)[:, :, slots],
+                in_=w_raw[g][:].bitcast(I32).rearrange("p a (b t w) -> p a t b w", t=SLOTS, b=BLOCKS)[:, :, slots],
             )
 
-        grouped = {}
-
-        def code_views(g, v):
-            src = c_raw[g, v // 2][:, :, N * (v % 2) : N * (v % 2 + 1)]
-            src = src.rearrange("p j (m e s) -> p m s e j", e=2, s=SLOTS)
-            dst = grouped["c", g, v][:].rearrange("p (s m e j) -> p m s e j", s=SLOTS, e=2, j=SLOTS)
-            return dst, src
+        c_words = {}
 
         def code_group(g, v):
-            grouped["c", g, v] = work.tile([P, SLOTS * N], BF16, name="c_grp", align_bytes=64, bufs=CGRP_BUFS)
-            dst, src = code_views(g, v)
-            nc.vector.tensor_copy(out=dst, in_=src)
-
-        def code_group_on_scalar(g, v, part):
-            if part == 0:
-                grouped["c", g, v] = work.tile([P, SLOTS * N], BF16, name="c_grp", align_bytes=64, bufs=CGRP_BUFS)
-            dst, src = code_views(g, v)
-            nc.scalar.copy(out=dst[:, 32 * part : 32 * (part + 1)], in_=src[:, 32 * part : 32 * (part + 1)])
+            c_words[g, v] = work.tile([P, SLOTS * N], BF16, name="c_grp", align_bytes=64, bufs=CODE_GROUP_BUFS)
+            nc.vector.tensor_copy(
+                out=c_words[g, v][:].rearrange("p (s m e t) -> p m s e t", s=SLOTS, e=2, t=SLOTS),
+                in_=c_raw[g, v][:].rearrange("p t (m e s) -> p m s e t", e=2, s=SLOTS),
+            )
 
         def code_quant(g, v):
-            nc.vector.quantize_mx(out=c_q[g][v][:].bitcast(FP8X4), scales=c_s[g][v][:], in_=grouped["c", g, v][:])
+            nc.vector.quantize_mx(out=c_q[g][v][:].bitcast(FP8X4), scales=c_s[g][v][:], in_=c_words[g, v][:])
 
         logits = {}
         soft = {}
         l16 = {}
+        l_words = {}
 
         def logit_mm(h, g, t):
-            z = bank()
-            logits[h, g, t] = z
+            logits[h, g, t] = bank()
             for a in range(D_PASSES):
                 nc.tensor.matmul_mx(
-                    out=z[:],
+                    out=logits[h, g, t][:],
                     lhsT=w_ord[g][:, a, 2 * P * t : 2 * P * (t + 1)].bitcast(FP4X4),
                     lhsT_scale=ws_ord[g][:, a, P * t : P * (t + 1)],
                     rhs=h_w[h][:, a, :].bitcast(FP4X4),
@@ -144,66 +145,60 @@ def tile_signed_bit_code_scores_k5_kernel(
                     stop=(a == D_PASSES - 1),
                 )
 
-        def logit_sig(h, g, t):
+        def logit_sigmoid(h, g, t):
             soft[h, g, t] = work.tile([P, N], F32, name="soft", bufs=SOFT_BUFS)
             nc.scalar.activation(out=soft[h, g, t][:], in_=logits[h, g, t][:], func=ACT.Sigmoid)
 
-        def logit_keep(h, g, t, on_vector):
-            saved = work.tile([P, N], F32, name="saved", bufs=SAVED_BUFS)
-            if on_vector:
-                nc.vector.tensor_copy(out=saved[:], in_=logits[h, g, t][:])
-            else:
-                nc.scalar.copy(out=saved[:], in_=logits[h, g, t][:])
+        def logit_save(h, g, t):
+            saved = work.tile([P, N], F32, name="saved", bufs=SAVED_BANKS)
+            nc.scalar.copy(out=saved[:], in_=logits[h, g, t][:])
             logits[h, g, t] = saved
 
         def logit_ln(h, g, t):
             nc.scalar.activation(out=soft[h, g, t][:], in_=soft[h, g, t][:], func=ACT.Ln, bias=FLOOR)
 
         def l_min(h, g, t):
-            nc.vector.tensor_tensor(
-                out=soft[h, g, t][:], in0=logits[h, g, t][:], in1=soft[h, g, t][:], op=ALU.min
-            )
+            nc.vector.tensor_tensor(out=soft[h, g, t][:], in0=logits[h, g, t][:], in1=soft[h, g, t][:], op=ALU.min)
 
-        def l_scale(h, g, t, on_gpsimd):
+        def l_scale(h, g, t, engine):
             if (h, g) not in l16:
                 l16[h, g] = work.tile([P, SLOTS, N], BF16, name="l16")
             col = SLOTS * g + t
-            (nc.gpsimd if on_gpsimd else nc.vector).tensor_scalar(
-                out=l16[h, g][:, t, :], in0=soft[h, g, t][:], scalar1=bw_pos[:, col : col + 1], scalar2=0.0,
+            engine.tensor_scalar(
+                out=l16[h, g][:, t, :], in0=soft[h, g, t][:], scalar1=bw_cols[:, col : col + 1], scalar2=0.0,
                 op0=ALU.mult, op1=ALU.add,
             )
 
         def interleave(dst, src, cols):
             nc.vector.tensor_copy(
-                out=dst[:, SLOTS * cols.start : SLOTS * cols.stop].rearrange("p (c i t) -> p c t i", i=4, t=SLOTS),
-                in_=src[:, :, cols].rearrange("p t (c i) -> p c t i", i=4),
+                out=dst[:, SLOTS * cols.start : SLOTS * cols.stop].rearrange("p (c i x) -> p c x i", i=4, x=SLOTS),
+                in_=src[:, :, cols].rearrange("p x (c i) -> p c x i", i=4),
             )
 
         def l_group(h, g):
-            grouped["l", h, g] = work.tile([P, SLOTS * N], BF16, name="l_grp", align_bytes=64)
-            interleave(grouped["l", h, g], l16[h, g], slice(0, N))
+            l_words[h, g] = work.tile([P, SLOTS * N], BF16, name="l_grp", align_bytes=64)
+            interleave(l_words[h, g], l16[h, g], slice(0, N))
 
         def l_quant(h, g):
-            nc.vector.quantize_mx(out=l_q[h][g][:].bitcast(FP8X4), scales=l_s[h][g][:], in_=grouped["l", h, g][:])
+            nc.vector.quantize_mx(out=l_q[h][g][:].bitcast(FP8X4), scales=l_s[h][g][:], in_=l_words[h, g][:])
 
         sums = {}
         y_t = {}
         turned = {}
-        y_out = {}
         y_words = {}
+        y_q = {}
 
         def score_mm(h, v, s):
-            acc = bank()
-            sums[h, v, s] = acc
-            for g in range(B_PASSES):
+            sums[h, v, s] = bank()
+            for g in range(BIT_GROUPS):
                 nc.tensor.matmul_mx(
-                    out=acc[:],
+                    out=sums[h, v, s][:],
                     lhsT=c_q[g][v][:, P * s : P * (s + 1)].bitcast(FP8X4),
                     lhsT_scale=c_s[g][v][:, P * s : P * (s + 1)],
                     rhs=l_q[h][g][:].bitcast(FP8X4),
                     rhs_scale=l_s[h][g][:],
                     start=(g == 0),
-                    stop=(g == B_PASSES - 1),
+                    stop=(g == BIT_GROUPS - 1),
                 )
 
         def score_affine(h, v, s, on_vector):
@@ -229,44 +224,46 @@ def tile_signed_bit_code_scores_k5_kernel(
                 )
 
         def y_drain(h, v, j, on_vector):
-            y_out[h, v, j] = work.tile([P, N], F32, name="y_out", bufs=10)
-            dst = y_out[h, v, j][:].rearrange("k (p s) -> k p s", s=SLOTS)
+            y_out = work.tile([P, N], F32, name="y_out", bufs=Y_OUT_BUFS)
+            dst = y_out[:].rearrange("k (p s) -> k p s", s=SLOTS)
             src = turned[h, v, j][:].rearrange("k (s p) -> k p s", s=SLOTS)
             if on_vector:
                 nc.vector.tensor_copy(out=dst, in_=src)
             else:
                 nc.scalar.copy(out=dst, in_=src)
             rows = slice(N * h + P * j, N * h + P * (j + 1))
-            nc.sync.dma_start(out=out_0[rows, N * v : N * (v + 1)], in_=y_out[h, v, j][:])
+            nc.sync.dma_start(out=out_0[rows, N * v : N * (v + 1)], in_=y_out[:])
 
-        def y_group_shared(h, v):
-            grouped["y", h, v] = work.tile([P, SLOTS * N], BF16, name="y_grp", align_bytes=64, bufs=3)
+        def y_words_tile(h, v):
+            y_words[h, v] = work.tile([P, SLOTS * N], BF16, name="y_grp", align_bytes=64, bufs=Y_PLANE_BUFS)
+
+        def y_group(h, v):
+            y_words_tile(h, v)
+            interleave(y_words[h, v], y_t[h, v], slice(0, N))
+
+        def y_group_gpsimd_part(h, v):
+            y_words_tile(h, v)
             nc.gpsimd.tensor_scalar(
-                out=grouped["y", h, v][:, 0 : SLOTS * SHARED].rearrange("p (c t) -> p c t", t=SLOTS),
-                in0=y_t[h, v][:, :, 0:SHARED].rearrange("p t c -> p c t"),
+                out=y_words[h, v][:, 0 : SLOTS * GPSIMD_COLUMNS].rearrange("p (c s) -> p c s", s=SLOTS),
+                in0=y_t[h, v][:, :, 0:GPSIMD_COLUMNS].rearrange("p s c -> p c s"),
                 scalar1=1.0, scalar2=0.0, op0=ALU.mult, op1=ALU.add,
             )
 
-        def y_group(h, v, first=0):
-            if first == 0:
-                grouped["y", h, v] = work.tile([P, SLOTS * N], BF16, name="y_grp", align_bytes=64, bufs=3)
-            if first < N:
-                interleave(grouped["y", h, v], y_t[h, v], slice(first, N))
+        def y_group_vector_part(h, v):
+            interleave(y_words[h, v], y_t[h, v], slice(GPSIMD_COLUMNS, N))
 
         def y_quant(h, v):
-            words = work.tile([P, N], U32, name="y_words", align_bytes=64, bufs=3)
-            y_words[h, v] = words
+            y_q[h, v] = work.tile([P, N], U32, name="y_words", align_bytes=64, bufs=Y_PLANE_BUFS)
             nc.vector.quantize_mx(
-                out=words[:].bitcast(FP8X4), scales=y_s[h][SLOTS * v : P, :], in_=grouped["y", h, v][:]
+                out=y_q[h, v][:].bitcast(FP8X4), scales=y_s[h][SLOTS * v : P, :], in_=y_words[h, v][:]
             )
 
         def store_words(h, v):
-            words = y_words[h, v]
-            dst = out_1[v].rearrange("p m t -> p (m t)")[:, SLOTS * N * h : SLOTS * N * (h + 1)]
-            nc.sync.dma_start(out=dst.bitcast(I32), in_=words[:].bitcast(I32))
+            dst = out_1[v].rearrange("p c s -> p (c s)")[:, SLOTS * N * h : SLOTS * N * (h + 1)]
+            nc.sync.dma_start(out=dst.bitcast(I32), in_=y_q[h, v][:].bitcast(I32))
 
         def store_scales(h):
-            for q in range(4):
+            for q in range(QUADRANTS):
                 nc.sync.dma_start(
                     out=out_2[:, 4 * q : 4 * q + 4, N * h : N * (h + 1)].bitcast(I32),
                     in_=y_s[h][32 * q : 32 * q + 16, :].bitcast(I32),
@@ -284,21 +281,21 @@ def tile_signed_bit_code_scores_k5_kernel(
         load_scales(ws_raw[0], w_scales, 0)
         load_words(h_w[0], h_words, 0)
         load_scales(h_s[0], h_scales, 0)
-        load_code(0, 0, slice(0, N))
+        load_code(0, 0)
         load_words(w_raw[1], w_words, 1)
         load_scales(ws_raw[1], w_scales, 1)
-        load_code(1, 0, slice(0, N))
-        load_code(0, 0, slice(N, 2 * N))
-        for g in range(B_PASSES):
-            rows = bit_weight[N * g : N * (g + 1)].rearrange("(q t r) -> t q r", t=SLOTS, r=8)
-            nc.sync.dma_start(
-                out=bw_rows[SLOTS * g : SLOTS * (g + 1), :].rearrange("t (q r) -> t q r", r=8), in_=rows
-            )
-        load_code(1, 0, slice(N, 2 * N))
+        load_code(1, 0)
         load_code(0, 1)
+        for g in range(BIT_GROUPS):
+            rows = bit_weight[N * g : N * (g + 1)].rearrange("(b t r) -> t b r", t=SLOTS, r=RUN)
+            nc.sync.dma_start(
+                out=bw_rows[SLOTS * g : SLOTS * (g + 1), :].rearrange("t (b r) -> t b r", r=RUN), in_=rows
+            )
+        load_code(1, 1)
+        load_code(0, 2, 3)
         load_words(h_w[1], h_words, 1)
         load_scales(h_s[1], h_scales, 1)
-        load_code(1, 1)
+        load_code(1, 2, 3)
         nc.sync.dma_start(out=scale16[:], in_=token_scale.rearrange("(v p s) -> p v s", p=P, s=SLOTS))
         nc.sync.dma_start(out=bias16[:], in_=token_bias.rearrange("(v p s) -> p v s", p=P, s=SLOTS))
         make_identity(nc, ident[:])
@@ -308,7 +305,7 @@ def tile_signed_bit_code_scores_k5_kernel(
         order_words(0, slice(2, SLOTS))
 
         bw_bank = bank()
-        for a in range(WARM):
+        for a in range(WARM_PASSES):
             nc.tensor.matmul_mx(
                 out=bw_bank[:],
                 lhsT=w_raw[0][:, a, 0 : 2 * P].bitcast(FP4X4),
@@ -319,102 +316,101 @@ def tile_signed_bit_code_scores_k5_kernel(
                 stop=True,
             )
 
-        def bit_weights():
-            nc.tensor.transpose(bw_bank[:, 0:P], bw_rows32[:], ident[:])
-            nc.vector.tensor_copy(out=bw_pos[:], in_=bw_bank[:, 0 : B_PASSES * SLOTS])
-
-        units = [(g, t) for g in range(B_PASSES) for t in range(SLOTS)]
+        slots_of_bits = [(g, t) for g in range(BIT_GROUPS) for t in range(SLOTS)]
         code_group(0, 0)
         order_words(1, slice(0, SLOTS))
         code_quant(0, 0)
         order_scales(1)
         code_group(1, 0)
+        code_group(0, 1)
         nc.vector.tensor_copy(out=bw_rows32[:], in_=bw_rows[:])
         code_quant(1, 0)
-        for i, (g, t) in enumerate(units):
+        for i, (g, t) in enumerate(slots_of_bits):
             logit_mm(0, g, t)
-            logit_sig(0, g, t)
-            if i < KEEP_A:
-                logit_keep(0, g, t, on_vector=False)
-            if i == 4:
-                bit_weights()
-            if i in (3, 5):
-                code_group_on_scalar(0, 1, (i - 3) // 2)
+            logit_sigmoid(0, g, t)
+            if i < SAVED_BANKS:
+                logit_save(0, g, t)
+            if i == BANKS - 3:
+                nc.tensor.transpose(bw_bank[:, 0:P], bw_rows32[:], ident[:])
+                nc.vector.tensor_copy(out=bw_cols[:], in_=bw_bank[:, 0 : BIT_GROUPS * SLOTS])
         code_group(1, 1)
+        code_quant(0, 1)
         code_group(0, 2)
         code_quant(1, 1)
         code_group(0, 3)
-        code_quant(0, 1)
         code_quant(0, 2)
-        code_quant(0, 3)
-        for g, t in units[:KEEP_A]:
+
+        for g, t in slots_of_bits[:SAVED_BANKS]:
             logit_mm(1, g, t)
-        for i, (g, t) in enumerate(units[KEEP_A:]):
+        for g, t in slots_of_bits[SAVED_BANKS:]:
             logit_ln(0, g, t)
             l_min(0, g, t)
-            if (g, t) != units[-1]:
-                l_scale(0, g, t, SCALE_G)
+            if (g, t) != slots_of_bits[-1]:
+                l_scale(0, g, t, nc.gpsimd)
             logit_mm(1, g, t)
-        for g, t in units[:KEEP_A]:
+        for g, t in slots_of_bits[:SAVED_BANKS]:
             logit_ln(0, g, t)
             l_min(0, g, t)
         nc.vector.tensor_copy(out=scale32[:], in_=scale16[:])
         nc.vector.tensor_copy(out=bias32[:], in_=bias16[:])
-        for g, t in units[-1:] + units[:KEEP_A]:
-            l_scale(0, g, t, False)
+        for g, t in slots_of_bits[-1:] + slots_of_bits[:SAVED_BANKS]:
+            l_scale(0, g, t, nc.vector)
         l_group(0, 1)
         l_group(0, 0)
         l_quant(0, 1)
         l_quant(0, 0)
         code_group(1, 2)
         code_group(1, 3)
-        for i, (g, t) in enumerate(units):
-            logit_sig(1, g, t)
-        steps = [(h, v) for h in range(HALVES) for v in range(V_GROUPS)]
-        AFF_V = (1,2,3)
-        DR_V = (0,1,2)
-        for i, (g, t) in enumerate(units):
+
+        for g, t in slots_of_bits:
+            logit_sigmoid(1, g, t)
+        for i, (g, t) in enumerate(slots_of_bits):
             logit_ln(1, g, t)
             l_min(1, g, t)
-            if i < len(units) - 1:
-                l_scale(1, g, t, SCALE_G)
+            if (g, t) != slots_of_bits[-1]:
+                l_scale(1, g, t, nc.gpsimd)
             if i < SLOTS:
                 score_mm(0, 0, i)
         for s in range(SLOTS):
             score_affine(0, 0, s, on_vector=False)
-        l_scale(1, 1, 3, False)
+        l_scale(1, *slots_of_bits[-1], nc.vector)
         code_quant(1, 2)
         l_group(1, 0)
+        code_quant(0, 3)
         code_quant(1, 3)
         y_group(0, 0)
         l_quant(1, 0)
+
+        steps = [(h, v) for h in range(HALVES) for v in range(TOKEN_GROUPS)]
         for i in range(1, len(steps) - 1):
-            now = steps[i]
-            last = steps[i - 1]
+            now, last = steps[i], steps[i - 1]
+            shared = i >= FIRST_SHARED_STEP
+            last_quant_is_due = i <= FIRST_SHARED_STEP
             for s in range(SLOTS):
                 score_mm(*now, s)
                 score_affine(*now, s, on_vector=False)
-            if i <= FIRST_SHARED:
+            if last_quant_is_due:
                 y_quant(*last)
             if i == 1:
                 l_group(1, 1)
-            if i < FIRST_SHARED:
-                y_group(*now)
+            if shared:
+                y_group_gpsimd_part(*now)
             else:
-                y_group_shared(*now)
+                y_group(*now)
             if i == 1:
                 l_quant(1, 1)
             for j in range(SLOTS):
                 y_turn(*last, j)
-                y_drain(*last, j, on_vector=(i >= FIRST_SHARED and j in DR_V))
-            if i <= FIRST_SHARED:
+                y_drain(*last, j, on_vector=(shared and j < VECTOR_DRAINS))
+            if last_quant_is_due:
                 store_words(*last)
-            if i >= FIRST_SHARED:
-                y_group(*now, SHARED)
+            if shared:
+                y_group_vector_part(*now)
                 y_quant(*now)
                 store_words(*now)
-            if now == (0, V_GROUPS - 1):
+            if now == (0, TOKEN_GROUPS - 1):
                 store_scales(0)
+
         last, now = steps[-2], steps[-1]
         for pair in ((0, 1), (2, 3)):
             for j in pair:
@@ -424,7 +420,7 @@ def tile_signed_bit_code_scores_k5_kernel(
             for j in pair:
                 y_drain(*last, j, on_vector=False)
             for s in pair:
-                score_affine(*now, s, on_vector=(s in AFF_V))
+                score_affine(*now, s, on_vector=(s > 0))
         y_group(*now)
         for j in range(2):
             y_turn(*now, j)

from contextlib import ExitStack

import concourse.mybir as mybir
from concourse.masks import make_identity

T, D, B, V = 1024, 2048, 1024, 2048
FLOPS = 2 * T * D * B + 2 * T * B * V

F32 = mybir.dt.float32
BF16 = mybir.dt.bfloat16
I32 = mybir.dt.int32
U32 = mybir.dt.uint32
U8 = mybir.dt.uint8
FP8X4 = mybir.dt.float8_e4m3fn_x4
FP4X4 = mybir.dt.float4_e2m1fn_x4
ACT = mybir.ActivationFunctionType
ALU = mybir.AluOpType

P = 128
N = 512
SLOTS = 4
BLOCKS = 16
RUN = 8
QUADRANTS = 4
D_PASSES = D // N
BIT_GROUPS = B // N
TOKEN_GROUPS = V // N
HALVES = T // N
BANKS = 8

FLOOR = 2.0**-58
WARM_PASSES = 3
SAVED_BANKS = 2
GPSIMD_COLUMNS = 320
FIRST_SHARED_STEP = 3
VECTOR_DRAINS = 3

SOFT_BUFS = 12
CODE_GROUP_BUFS = 4
WIDE_BUFS = 6
Y_OUT_BUFS = 10
Y_PLANE_BUFS = 3


def tile_signed_bit_code_scores_k5_kernel(
    tc, h_words, h_scales, w_words, w_scales, bit_weight, code, token_scale, token_bias, out_0, out_1, out_2
):
    nc = tc.nc
    with ExitStack() as ctx:
        keep = ctx.enter_context(tc.tile_pool(name="keep", bufs=1))
        work = ctx.enter_context(tc.tile_pool(name="work", bufs=2))
        psum = ctx.enter_context(tc.psum_pool(name="psum", bufs=BANKS))
        ctx.enter_context(tc.manual_schedule())

        def kept(name, shape, dtype):
            return keep.tile(shape, dtype, name=name, align_bytes=64)

        def bank():
            return psum.tile([P, N], F32, name="bank")

        w_raw = [kept("w_raw%d" % g, [P, D_PASSES, 2 * N], U8) for g in range(BIT_GROUPS)]
        ws_raw = [kept("ws_raw%d" % g, [P, D_PASSES, N], U8) for g in range(BIT_GROUPS)]
        w_ord = [kept("w_ord%d" % g, [P, D_PASSES, 2 * N], U8) for g in range(BIT_GROUPS)]
        ws_ord = [kept("ws_ord%d" % g, [P, D_PASSES, N], U8) for g in range(BIT_GROUPS)]
        h_w = [kept("h_w%d" % h, [P, D_PASSES, 2 * N], U8) for h in range(HALVES)]
        h_s = [kept("h_s%d" % h, [P, D_PASSES, N], U8) for h in range(HALVES)]
        c_raw = {}
        for g in range(BIT_GROUPS):
            for v in range(2):
                c_raw[g, v] = kept("c_raw%d_%d" % (g, v), [P, SLOTS, N], BF16)
            late = work.tile([P, SLOTS, 2 * N], BF16, name="c_late", tag="wide", bufs=WIDE_BUFS)
            c_raw[g, 2, 3] = late
            c_raw[g, 2] = late[:, :, 0:N]
            c_raw[g, 3] = late[:, :, N : 2 * N]
        c_q = [[kept("c_q%d_%d" % (g, v), [P, N], U32) for v in range(TOKEN_GROUPS)] for g in range(BIT_GROUPS)]
        c_s = [[kept("c_s%d_%d" % (g, v), [P, N], U8) for v in range(TOKEN_GROUPS)] for g in range(BIT_GROUPS)]
        l_q = [[kept("l_q%d_%d" % (h, g), [P, N], U32) for g in range(BIT_GROUPS)] for h in range(HALVES)]
        l_s = [[kept("l_s%d_%d" % (h, g), [P, N], U8) for g in range(BIT_GROUPS)] for h in range(HALVES)]
        y_s = [kept("y_s%d" % h, [P, N], U8) for h in range(HALVES)]
        ident = kept("ident", [P, P], F32)
        bw_rows = kept("bw_rows", [P, P], BF16)
        bw_rows32 = kept("bw_rows32", [P, P], F32)
        bw_cols = kept("bw_cols", [P, BIT_GROUPS * SLOTS], F32)
        scale16 = kept("scale16", [P, TOKEN_GROUPS, SLOTS], BF16)
        bias16 = kept("bias16", [P, TOKEN_GROUPS, SLOTS], BF16)
        scale32 = kept("scale32", [P, TOKEN_GROUPS, SLOTS], F32)
        bias32 = kept("bias32", [P, TOKEN_GROUPS, SLOTS], F32)
        warm_in = kept("warm_in", [P, 1], F32)
        warm_out = kept("warm_out", [P, 1], F32)

        def load_words(dst, src, part):
            view = src[:, :, 2 * N * part : 2 * N * (part + 1)].rearrange("a p c -> p a c")
            nc.sync.dma_start(out=dst[:].bitcast(I32), in_=view.bitcast(I32))

        def load_scales(dst, src, part):
            for q in range(QUADRANTS):
                view = src[:, 4 * q : 4 * q + 4, N * part : N * (part + 1)].rearrange("a r c -> r a c")
                nc.sync.dma_start(out=dst[32 * q : 32 * q + 4, :, :].bitcast(I32), in_=view.bitcast(I32))

        def load_code(g, *token_groups):
            rows = code[N * g : N * (g + 1), N * token_groups[0] : N * (token_groups[-1] + 1)]
            rows = rows.rearrange("(b t r) c -> t b r c", t=SLOTS, r=RUN)
            for t in range(SLOTS):
                nc.sync.dma_start(out=c_raw[(g, *token_groups)][:, t, :], in_=rows[t])

        def order_scales(g):
            nc.vector.tensor_copy(
                out=ws_ord[g][:].bitcast(I32).rearrange("p a (t b w) -> p a t b w", t=SLOTS, b=BLOCKS),
                in_=ws_raw[g][:].bitcast(I32).rearrange("p a (b t w) -> p a t b w", t=SLOTS, b=BLOCKS),
            )

        def order_words(g, slots):
            nc.vector.tensor_copy(
                out=w_ord[g][:].bitcast(I32).rearrange("p a (t b w) -> p a t b w", t=SLOTS, b=BLOCKS)[:, :, slots],
                in_=w_raw[g][:].bitcast(I32).rearrange("p a (b t w) -> p a t b w", t=SLOTS, b=BLOCKS)[:, :, slots],
            )

        c_words = {}

        def code_group(g, v):
            c_words[g, v] = work.tile([P, SLOTS * N], BF16, name="c_grp", align_bytes=64, bufs=CODE_GROUP_BUFS)
            nc.vector.tensor_copy(
                out=c_words[g, v][:].rearrange("p (s m e t) -> p m s e t", s=SLOTS, e=2, t=SLOTS),
                in_=c_raw[g, v][:].rearrange("p t (m e s) -> p m s e t", e=2, s=SLOTS),
            )

        def code_quant(g, v):
            nc.vector.quantize_mx(out=c_q[g][v][:].bitcast(FP8X4), scales=c_s[g][v][:], in_=c_words[g, v][:])

        logits = {}
        soft = {}
        l16 = {}
        l_words = {}

        def logit_mm(h, g, t):
            logits[h, g, t] = bank()
            for a in range(D_PASSES):
                nc.tensor.matmul_mx(
                    out=logits[h, g, t][:],
                    lhsT=w_ord[g][:, a, 2 * P * t : 2 * P * (t + 1)].bitcast(FP4X4),
                    lhsT_scale=ws_ord[g][:, a, P * t : P * (t + 1)],
                    rhs=h_w[h][:, a, :].bitcast(FP4X4),
                    rhs_scale=h_s[h][:, a, :],
                    start=(a == 0),
                    stop=(a == D_PASSES - 1),
                )

        def logit_sigmoid(h, g, t):
            soft[h, g, t] = work.tile([P, N], F32, name="soft", bufs=SOFT_BUFS)
            nc.scalar.activation(out=soft[h, g, t][:], in_=logits[h, g, t][:], func=ACT.Sigmoid)

        def logit_save(h, g, t):
            saved = work.tile([P, N], F32, name="saved", bufs=SAVED_BANKS)
            nc.scalar.copy(out=saved[:], in_=logits[h, g, t][:])
            logits[h, g, t] = saved

        def logit_ln(h, g, t):
            nc.scalar.activation(out=soft[h, g, t][:], in_=soft[h, g, t][:], func=ACT.Ln, bias=FLOOR)

        def l_min(h, g, t):
            nc.vector.tensor_tensor(out=soft[h, g, t][:], in0=logits[h, g, t][:], in1=soft[h, g, t][:], op=ALU.min)

        def l_scale(h, g, t, engine):
            if (h, g) not in l16:
                l16[h, g] = work.tile([P, SLOTS, N], BF16, name="l16")
            col = SLOTS * g + t
            engine.tensor_scalar(
                out=l16[h, g][:, t, :], in0=soft[h, g, t][:], scalar1=bw_cols[:, col : col + 1], scalar2=0.0,
                op0=ALU.mult, op1=ALU.add,
            )

        def interleave(dst, src, cols):
            nc.vector.tensor_copy(
                out=dst[:, SLOTS * cols.start : SLOTS * cols.stop].rearrange("p (c i x) -> p c x i", i=4, x=SLOTS),
                in_=src[:, :, cols].rearrange("p x (c i) -> p c x i", i=4),
            )

        def l_group(h, g):
            l_words[h, g] = work.tile([P, SLOTS * N], BF16, name="l_grp", align_bytes=64)
            interleave(l_words[h, g], l16[h, g], slice(0, N))

        def l_quant(h, g):
            nc.vector.quantize_mx(out=l_q[h][g][:].bitcast(FP8X4), scales=l_s[h][g][:], in_=l_words[h, g][:])

        sums = {}
        y_t = {}
        turned = {}
        y_words = {}
        y_q = {}

        def score_mm(h, v, s):
            sums[h, v, s] = bank()
            for g in range(BIT_GROUPS):
                nc.tensor.matmul_mx(
                    out=sums[h, v, s][:],
                    lhsT=c_q[g][v][:, P * s : P * (s + 1)].bitcast(FP8X4),
                    lhsT_scale=c_s[g][v][:, P * s : P * (s + 1)],
                    rhs=l_q[h][g][:].bitcast(FP8X4),
                    rhs_scale=l_s[h][g][:],
                    start=(g == 0),
                    stop=(g == BIT_GROUPS - 1),
                )

        def score_affine(h, v, s, on_vector):
            if s == 0:
                y_t[h, v] = work.tile([P, SLOTS, N], F32, name="y_t", tag="wide", bufs=WIDE_BUFS)
            dst = y_t[h, v][:, s, :]
            if on_vector:
                nc.vector.tensor_scalar(
                    out=dst, in0=sums[h, v, s][:], scalar1=scale32[:, v, s : s + 1], scalar2=bias32[:, v, s : s + 1],
                    op0=ALU.mult, op1=ALU.add,
                )
            else:
                nc.scalar.activation(
                    out=dst, in_=sums[h, v, s][:], func=ACT.Identity,
                    scale=scale32[:, v, s : s + 1], bias=bias32[:, v, s : s + 1],
                )

        def y_turn(h, v, j):
            turned[h, v, j] = bank()
            for s in range(SLOTS):
                nc.tensor.transpose(
                    turned[h, v, j][:, P * s : P * (s + 1)], y_t[h, v][:, s, P * j : P * (j + 1)], ident[:]
                )

        def y_drain(h, v, j, on_vector):
            y_out = work.tile([P, N], F32, name="y_out", bufs=Y_OUT_BUFS)
            dst = y_out[:].rearrange("k (p s) -> k p s", s=SLOTS)
            src = turned[h, v, j][:].rearrange("k (s p) -> k p s", s=SLOTS)
            if on_vector:
                nc.vector.tensor_copy(out=dst, in_=src)
            else:
                nc.scalar.copy(out=dst, in_=src)
            rows = slice(N * h + P * j, N * h + P * (j + 1))
            nc.sync.dma_start(out=out_0[rows, N * v : N * (v + 1)], in_=y_out[:])

        def y_words_tile(h, v):
            y_words[h, v] = work.tile([P, SLOTS * N], BF16, name="y_grp", align_bytes=64, bufs=Y_PLANE_BUFS)

        def y_group(h, v):
            y_words_tile(h, v)
            interleave(y_words[h, v], y_t[h, v], slice(0, N))

        def y_group_gpsimd_part(h, v):
            y_words_tile(h, v)
            nc.gpsimd.tensor_scalar(
                out=y_words[h, v][:, 0 : SLOTS * GPSIMD_COLUMNS].rearrange("p (c s) -> p c s", s=SLOTS),
                in0=y_t[h, v][:, :, 0:GPSIMD_COLUMNS].rearrange("p s c -> p c s"),
                scalar1=1.0, scalar2=0.0, op0=ALU.mult, op1=ALU.add,
            )

        def y_group_vector_part(h, v):
            interleave(y_words[h, v], y_t[h, v], slice(GPSIMD_COLUMNS, N))

        def y_quant(h, v):
            y_q[h, v] = work.tile([P, N], U32, name="y_words", align_bytes=64, bufs=Y_PLANE_BUFS)
            nc.vector.quantize_mx(
                out=y_q[h, v][:].bitcast(FP8X4), scales=y_s[h][SLOTS * v : P, :], in_=y_words[h, v][:]
            )

        def store_words(h, v):
            dst = out_1[v].rearrange("p c s -> p (c s)")[:, SLOTS * N * h : SLOTS * N * (h + 1)]
            nc.sync.dma_start(out=dst.bitcast(I32), in_=y_q[h, v][:].bitcast(I32))

        def store_scales(h):
            for q in range(QUADRANTS):
                nc.sync.dma_start(
                    out=out_2[:, 4 * q : 4 * q + 4, N * h : N * (h + 1)].bitcast(I32),
                    in_=y_s[h][32 * q : 32 * q + 16, :].bitcast(I32),
                )

        nc.vector.memset(ws_raw[0][:].bitcast(I32), 0)
        nc.vector.memset(h_s[0][:].bitcast(I32), 0)
        nc.vector.memset(warm_in[:], 0.0)
        nc.vector.memset(ws_raw[1][:].bitcast(I32), 0)
        nc.vector.memset(h_s[1][:].bitcast(I32), 0)
        nc.vector.memset(bw_rows[:], 0.0)
        nc.scalar.activation(out=warm_out[:], in_=warm_in[:], func=ACT.Sigmoid)

        load_words(w_raw[0], w_words, 0)
        load_scales(ws_raw[0], w_scales, 0)
        load_words(h_w[0], h_words, 0)
        load_scales(h_s[0], h_scales, 0)
        load_code(0, 0)
        load_words(w_raw[1], w_words, 1)
        load_scales(ws_raw[1], w_scales, 1)
        load_code(1, 0)
        load_code(0, 1)
        for g in range(BIT_GROUPS):
            rows = bit_weight[N * g : N * (g + 1)].rearrange("(b t r) -> t b r", t=SLOTS, r=RUN)
            nc.sync.dma_start(
                out=bw_rows[SLOTS * g : SLOTS * (g + 1), :].rearrange("t (b r) -> t b r", r=RUN), in_=rows
            )
        load_code(1, 1)
        load_code(0, 2, 3)
        load_words(h_w[1], h_words, 1)
        load_scales(h_s[1], h_scales, 1)
        load_code(1, 2, 3)
        nc.sync.dma_start(out=scale16[:], in_=token_scale.rearrange("(v p s) -> p v s", p=P, s=SLOTS))
        nc.sync.dma_start(out=bias16[:], in_=token_bias.rearrange("(v p s) -> p v s", p=P, s=SLOTS))
        make_identity(nc, ident[:])

        order_words(0, slice(0, 2))
        order_scales(0)
        order_words(0, slice(2, SLOTS))

        bw_bank = bank()
        for a in range(WARM_PASSES):
            nc.tensor.matmul_mx(
                out=bw_bank[:],
                lhsT=w_raw[0][:, a, 0 : 2 * P].bitcast(FP4X4),
                lhsT_scale=ws_raw[0][:, a, 0:P],
                rhs=w_raw[0][:, a, :].bitcast(FP4X4),
                rhs_scale=ws_raw[0][:, a, :],
                start=True,
                stop=True,
            )

        slots_of_bits = [(g, t) for g in range(BIT_GROUPS) for t in range(SLOTS)]
        code_group(0, 0)
        order_words(1, slice(0, SLOTS))
        code_quant(0, 0)
        order_scales(1)
        code_group(1, 0)
        code_group(0, 1)
        nc.vector.tensor_copy(out=bw_rows32[:], in_=bw_rows[:])
        code_quant(1, 0)
        for i, (g, t) in enumerate(slots_of_bits):
            logit_mm(0, g, t)
            logit_sigmoid(0, g, t)
            if i < SAVED_BANKS:
                logit_save(0, g, t)
            if i == BANKS - 3:
                nc.tensor.transpose(bw_bank[:, 0:P], bw_rows32[:], ident[:])
                nc.vector.tensor_copy(out=bw_cols[:], in_=bw_bank[:, 0 : BIT_GROUPS * SLOTS])
        code_group(1, 1)
        code_quant(0, 1)
        code_group(0, 2)
        code_quant(1, 1)
        code_group(0, 3)
        code_quant(0, 2)

        for g, t in slots_of_bits[:SAVED_BANKS]:
            logit_mm(1, g, t)
        for g, t in slots_of_bits[SAVED_BANKS:]:
            logit_ln(0, g, t)
            l_min(0, g, t)
            if (g, t) != slots_of_bits[-1]:
                l_scale(0, g, t, nc.gpsimd)
            logit_mm(1, g, t)
        for g, t in slots_of_bits[:SAVED_BANKS]:
            logit_ln(0, g, t)
            l_min(0, g, t)
        nc.vector.tensor_copy(out=scale32[:], in_=scale16[:])
        nc.vector.tensor_copy(out=bias32[:], in_=bias16[:])
        for g, t in slots_of_bits[-1:] + slots_of_bits[:SAVED_BANKS]:
            l_scale(0, g, t, nc.vector)
        l_group(0, 1)
        l_group(0, 0)
        l_quant(0, 1)
        l_quant(0, 0)
        code_group(1, 2)
        code_group(1, 3)

        for g, t in slots_of_bits:
            logit_sigmoid(1, g, t)
        for i, (g, t) in enumerate(slots_of_bits):
            logit_ln(1, g, t)
            l_min(1, g, t)
            if (g, t) != slots_of_bits[-1]:
                l_scale(1, g, t, nc.gpsimd)
            if i < SLOTS:
                score_mm(0, 0, i)
        for s in range(SLOTS):
            score_affine(0, 0, s, on_vector=False)
        l_scale(1, *slots_of_bits[-1], nc.vector)
        code_quant(1, 2)
        l_group(1, 0)
        code_quant(0, 3)
        code_quant(1, 3)
        y_group(0, 0)
        l_quant(1, 0)

        steps = [(h, v) for h in range(HALVES) for v in range(TOKEN_GROUPS)]
        for i in range(1, len(steps) - 1):
            now, last = steps[i], steps[i - 1]
            shared = i >= FIRST_SHARED_STEP
            last_quant_is_due = i <= FIRST_SHARED_STEP
            for s in range(SLOTS):
                score_mm(*now, s)
                score_affine(*now, s, on_vector=False)
            if last_quant_is_due:
                y_quant(*last)
            if i == 1:
                l_group(1, 1)
            if shared:
                y_group_gpsimd_part(*now)
            else:
                y_group(*now)
            if i == 1:
                l_quant(1, 1)
            for j in range(SLOTS):
                y_turn(*last, j)
                y_drain(*last, j, on_vector=(shared and j < VECTOR_DRAINS))
            if last_quant_is_due:
                store_words(*last)
            if shared:
                y_group_vector_part(*now)
                y_quant(*now)
                store_words(*now)
            if now == (0, TOKEN_GROUPS - 1):
                store_scales(0)

        last, now = steps[-2], steps[-1]
        for pair in ((0, 1), (2, 3)):
            for j in pair:
                y_turn(*last, j)
            for s in pair:
                score_mm(*now, s)
            for j in pair:
                y_drain(*last, j, on_vector=False)
            for s in pair:
                score_affine(*now, s, on_vector=(s > 0))
        y_group(*now)
        for j in range(2):
            y_turn(*now, j)
            y_drain(*now, j, on_vector=False)
        y_quant(*now)
        y_turn(*now, 2)
        y_drain(*now, 2, on_vector=False)
        store_words(*now)
        y_turn(*now, 3)
        y_drain(*now, 3, on_vector=True)
        store_scales(1)
